import numpy as np
import ml_dtypes


def mxq(x, axis, fmt="e4m3"):
    dtype, down = {"e4m3": (ml_dtypes.float8_e4m3fn, 7), "e5m2": (ml_dtypes.float8_e5m2, 14)}[fmt]
    v = np.moveaxis(np.asarray(x, np.float32).astype(ml_dtypes.bfloat16).astype(np.float64), axis, -1)
    blocks = v.reshape(v.shape[:-1] + (-1, 32))
    amax = np.abs(blocks).max(-1, keepdims=True)
    byte = np.maximum(np.where(amax > 0, np.frexp(amax)[1] - 1 + 127, 0) - down, 1)
    scale = np.exp2(byte - 127.0)
    codes = (blocks / scale).astype(np.float32).astype(dtype).astype(np.float64)
    return np.moveaxis((codes * scale).reshape(v.shape), -1, axis)


WIDE = False


def mx_kscale(k):
    if not WIDE:
        return np.ones(k)
    levels = np.array([10, -10, 5, -5, 0])
    if k % 512:
        return np.exp2(np.random.permutation(np.resize(levels, k // 32))).repeat(32)
    a = np.empty((k // 512, 16))
    for p in range(k // 512):
        a[p, :8] = np.random.permutation(np.resize(levels, 8))
        for g in range(8):
            far = levels[np.abs(levels - a[p, g]) >= 10]
            a[p, g + 8] = far[np.random.randint(len(far))]
    return np.exp2(a.ravel()).repeat(32)


BF16 = ml_dtypes.bfloat16


def bf(x):
    return np.asarray(x, np.float32).astype(BF16)


def f64(x):
    return np.asarray(x).astype(np.float64)


E2M1 = np.array([0.0, 0.5, 1.0, 1.5, 2.0, 3.0, 4.0, 6.0, -0.0, -0.5, -1.0, -1.5, -2.0, -3.0, -4.0, -6.0])


def pack_weight(w, fmt):
    k, n = w.shape
    w = f64(bf(w)).reshape(k // 32, 32, n)
    amax = np.abs(w).max(1)
    if fmt == "e4m3":
        byte = np.frexp(amax)[1] - 1 + 127 - 7
    else:
        mant, ex = np.frexp(amax / 6.0)
        byte = np.where(mant > 0.5, ex, ex - 1) + 127
    byte = np.clip(np.where(amax > 0, byte, 1), 1, 254)
    scaled = (w * np.exp2(127.0 - byte)[:, None, :]).reshape(k, n).astype(np.float32)
    by_word = np.ascontiguousarray(scaled.reshape(k // 512, 128, 4, n).transpose(0, 1, 3, 2))
    if fmt == "e4m3":
        words = by_word.astype(ml_dtypes.float8_e4m3fn).view(np.uint8)
    else:
        c = by_word.astype(ml_dtypes.float4_e2m1fn).view(np.uint8) & 0xF
        words = c[..., 0::2] | (c[..., 1::2] << 4)
    return np.ascontiguousarray(words), np.ascontiguousarray(byte.astype(np.uint8).reshape(k // 512, 16, n))


def unpack_weight(words, scales, fmt):
    g, p, n, _ = words.shape
    if fmt == "e4m3":
        vals = np.ascontiguousarray(words).view(ml_dtypes.float8_e4m3fn).astype(np.float64)
    else:
        nib = np.empty((g, p, n, 4), np.uint8)
        nib[..., 0::2] = words & 0xF
        nib[..., 1::2] = words >> 4
        vals = E2M1[nib]
    vals = vals * np.repeat(np.exp2(scales.astype(np.float64) - 127.0), 8, axis=1)[..., None]
    return vals.transpose(0, 1, 3, 2).reshape(g * 512, n)
def pack4(w):
    words, scales = pack_weight(w, "e2m1")
    return words.reshape(words.shape[0], 128, -1), scales


def unpack4(words, scales):
    return unpack_weight(words.reshape(words.shape[0], 128, -1, 2), scales, "e2m1")


E4M3FN = np.array([(-1.0 if i & 128 else 1.0) * ((1.0 + (i & 7) / 8.0) * 2.0 ** (((i >> 3) & 15) - 7) if i & 120 else (i & 7) * 2.0 ** -9) for i in range(256)])


def e4m3fn_bytes(y):
    return np.clip(np.asarray(y, np.float64), -448.0, 448.0).astype(np.float32).astype(ml_dtypes.float8_e4m3fn).view(np.uint8)


def e4m3fn_values(b):
    return E4M3FN[b]


N, F, D, M = 1024, 1024, 1024, 1024


def draw0():
    p, q = mx_kscale(F), mx_kscale(D)
    x = bf(np.random.standard_normal((N, F)) * p)
    w_words, w_scales = pack4(np.random.standard_normal((F, D)) / np.sqrt(F) / p[:, None])
    c = bf(0.5 * np.random.standard_normal(D))
    g = bf((1.0 + 0.1 * np.random.standard_normal(D)) * q)
    a_words, a_scales = pack4(1.5 * np.random.standard_normal((D, M)) / np.sqrt(D) / q[:, None])
    s = bf(np.random.uniform(0.5, 2.0, M))
    return {"x": x, "w_words": w_words, "w_scales": w_scales, "c": c, "g": g, "a_words": a_words, "a_scales": a_scales, "s": s}


def _embed(x, w_words, w_scales, c, g):
    h = mxq(f64(x), 1, "e4m3") @ unpack4(w_words, w_scales)
    return np.tanh(h + f64(c)[None, :]) * f64(g)[None, :]


def core(x, w_words, w_scales, c, g, a_words, a_scales, s):
    z = _embed(x, w_words, w_scales, c, g)
    t = mxq(z, 1, "e4m3") @ unpack4(a_words, a_scales)
    sk = f64(s)
    u = sk[None, :] * t
    cos_u = np.cos(u)
    sin_u = np.sin(u)
    mc = np.mean(cos_u, axis=0)
    ms = np.mean(sin_u, axis=0)
    psi = np.exp(-sk * sk / 2.0)
    return 4.0 * sk[None, :] * (ms[None, :] * cos_u - (mc - psi)[None, :] * sin_u)


def setup_inputs():
    drawn = draw0()
    full = np.asarray(drawn['x']).astype(np.float64)
    scale = (np.abs(full).reshape(8, 128, 8, 128).max(axis=(1, 3)) / 448.0).astype(np.float32)
    given = {}
    for key, value in drawn.items():
        if key == 'x':
            given['x_bytes'] = e4m3fn_bytes(full / np.repeat(np.repeat(scale.astype(np.float64), 128, axis=0), 128, axis=1))
            given['x_scale'] = scale
        else:
            given[key] = value
    return given


def reference(x_bytes, x_scale, w_words, w_scales, c, g, a_words, a_scales, s):
    return core(e4m3fn_values(x_bytes) * np.repeat(np.repeat(x_scale.astype(np.float64), 128, axis=0), 128, axis=1), w_words, w_scales, c, g, a_words, a_scales, s)

@@ -1,0 +1,466 @@
+import math
+from contextlib import ExitStack
+
+import concourse.mybir as mybir
+from concourse.masks import make_identity
+
+N, F, D, M = 1024, 1024, 1024, 1024
+FLOPS = 2 * N * F * D + 2 * N * D * M
+
+F32 = mybir.dt.float32
+BF16 = mybir.dt.bfloat16
+I32 = mybir.dt.int32
+U32 = mybir.dt.uint32
+U8 = mybir.dt.uint8
+E4M3 = mybir.dt.float8_e4m3fn
+E4M3X4 = mybir.dt.float8_e4m3fn_x4
+E2M1X4 = mybir.dt.float4_e2m1fn_x4
+ALU = mybir.AluOpType
+ACT = mybir.ActivationFunctionType
+
+P = 128
+HALF = 512
+TWO_PI = 2.0 * math.pi
+
+
+def tile_lejepasigregrandomknotslicegrad_d2p_kernel(
+    tc, x_bytes, x_scale, w_words, w_scales, c, g, a_words, a_scales, s, out
+):
+    nc = tc.nc
+    with ExitStack() as ctx:
+        keep = ctx.enter_context(tc.tile_pool(name="keep", bufs=1))
+        work = ctx.enter_context(tc.tile_pool(name="work", bufs=2))
+        psum = ctx.enter_context(tc.psum_pool(name="psum", bufs=1))
+        ctx.enter_context(tc.manual_schedule())
+
+        warm = keep.tile([P, 1], F32, name="warm")
+        warm_out = keep.tile([P, 1], F32, name="warm_out")
+        nc.vector.memset(warm[:], 0.0)
+        wsc_raw = keep.tile([P, 2, D], U8, name="wsc_raw", align_bytes=64)
+        asc = keep.tile([P, 2, M], U8, name="asc", align_bytes=64)
+        nc.vector.memset(wsc_raw[:].bitcast(I32), 0)
+        s_rows = keep.tile([P, P], BF16, name="s_rows")
+        nc.gpsimd.memset(s_rows[:], 0.0)
+        ident = keep.tile([P, P], F32, name="ident")
+        make_identity(nc, ident[:])
+        nc.gpsimd.memset(asc[:].bitcast(I32), 0)
+
+        xs_all = keep.tile([P, 64], F32, name="xs_all")
+        nc.scalar.dma_start(out=xs_all[:], in_=x_scale.rearrange("i j -> (i j)").partition_broadcast(P))
+        nc.scalar.activation(out=warm_out[:], in_=warm[:], func=ACT.Silu)
+        c_b = keep.tile([P, 2, 4], BF16, name="c_b")
+        g_b = keep.tile([P, 2, 4], BF16, name="g_b")
+        nc.scalar.dma_start(out=s_rows[0:8, :], in_=s.rearrange("(j p) -> j p", p=P))
+        nc.scalar.dma_start(out=c_b[:], in_=c.rearrange("(q p t) -> p q t", p=P, t=4))
+        nc.scalar.dma_start(out=g_b[:], in_=g.rearrange("(q p t) -> p q t", p=P, t=4))
+
+        x_raw = []
+        for i in range(8):
+            x_raw_i = keep.tile([P, F], U8, name=f"x_raw{i}", align_bytes=64)
+            x_raw.append(x_raw_i)
+        w_raw = []
+        for q in range(2):
+            w_raw_q = keep.tile([P, 2, 1024], U8, name=f"w_raw{q}", align_bytes=64)
+            w_raw.append(w_raw_q)
+        a_raw = keep.tile([P, 2, 2 * M], U8, name="a_raw", align_bytes=64)
+
+        def load_x(i):
+            nc.sync.dma_start(out=x_raw[i][:], in_=x_bytes[P * i : P * (i + 1), :])
+
+        w_view = w_words.rearrange("k p b -> p k b")
+
+        def load_w(q):
+            nc.sync.dma_start(
+                out=w_raw[q][:].bitcast(I32), in_=w_view[:, :, 1024 * q : 1024 * (q + 1)].bitcast(I32)
+            )
+
+        def load_scales(tile, src):
+            for quad in range(4):
+                nc.sync.dma_start(
+                    out=tile[32 * quad : 32 * quad + 4].bitcast(I32),
+                    in_=src[:, 4 * quad : 4 * quad + 4, :].rearrange("k r n -> r k n").bitcast(I32),
+                )
+
+        load_w(0)
+        load_x(0)
+        load_x(1)
+        load_x(2)
+        load_scales(wsc_raw, w_scales)
+        load_x(3)
+        load_x(4)
+        load_w(1)
+        load_x(5)
+        load_x(6)
+        load_x(7)
+        nc.sync.dma_start(out=a_raw[:].bitcast(I32), in_=a_words.rearrange("k p b -> p k b").bitcast(I32))
+        load_scales(asc, a_scales)
+
+        xsc = keep.tile([P, 8, 2], F32, name="xsc")
+        xs_view = xs_all[:].rearrange("p (i k q) -> p i k q", i=8, k=2)
+        for quad in range(4):
+            rows = slice(32 * quad, 32 * quad + 32)
+            nc.gpsimd.tensor_copy(out=xsc[rows], in_=xs_view[rows, :, :, quad])
+        c_col = keep.tile([P, 2, 4], F32, name="c_col")
+        g_col = keep.tile([P, 2, 4], F32, name="g_col")
+        nc.gpsimd.tensor_copy(out=c_col[:], in_=c_b[:])
+        nc.gpsimd.tensor_copy(out=g_col[:], in_=g_b[:])
+
+        x_il, x_codes, x_planes = {}, {}, {}
+        for h in range(2):
+            for k in range(2):
+                xi = keep.tile([P, HALF, 4], BF16, name=f"x_il{h}{k}", align_bytes=64)
+                xc = keep.tile([P, HALF], U32, name=f"x_codes{h}{k}", align_bytes=64)
+                xp = keep.tile([P, HALF], U8, name=f"x_planes{h}{k}", align_bytes=64)
+                x_il[h, k], x_codes[h, k], x_planes[h, k] = xi, xc, xp
+        x_bf, x_t = {}, {}
+
+        def widen_x(i, on_scalar):
+            wide = work.tile([P, F], BF16, name="x_bf", bufs=6, align_bytes=64)
+            x_bf[i] = wide
+            if on_scalar:
+                nc.scalar.copy(out=wide[:], in_=x_raw[i][:].bitcast(E4M3))
+            else:
+                nc.vector.tensor_copy(out=wide[:], in_=x_raw[i][:].bitcast(E4M3))
+
+        def turn_x(i):
+            words = x_bf[i][:].bitcast(F32)
+            xt = psum.tile([P, 2, 2, P], F32, name="tp", bufs=3)
+            x_t[i] = xt
+            for k in range(2):
+                for u in range(2):
+                    nc.tensor.transpose(xt[:, k, u, :], words[:, 256 * k + u : 256 * (k + 1) : 2], ident[:])
+
+        def scale_x(i, k, on_scalar=False):
+            h, b = divmod(i, 4)
+            dst = x_il[h, k][:, P * b : P * (b + 1), :].rearrange("p n (u e) -> p n u e", e=2)
+            src = x_t[i][:, k].bitcast(BF16).rearrange("p u (n e) -> p n u e", e=2)
+            if on_scalar:
+                nc.scalar.activation(out=dst, in_=src, func=ACT.Copy, scale=xsc[:, i, k : k + 1])
+            else:
+                nc.vector.tensor_scalar(out=dst, in0=src, scalar1=xsc[:, i, k : k + 1], scalar2=None, op0=ALU.mult)
+
+        def quant_x(h, k):
+            nc.vector.quantize_mx(
+                out=x_codes[h, k][:].bitcast(E4M3X4),
+                scales=x_planes[h, k][:],
+                in_=x_il[h, k][:].rearrange("p n t -> p (n t)"),
+            )
+
+        w_perm = {}
+        wsc = []
+        for q in range(2):
+            wsc_q = keep.tile([P, 2, 4, P], U8, name=f"wsc{q}", align_bytes=64)
+            wsc.append(wsc_q)
+
+        def permute_w(q):
+            for k in range(2):
+                wp = keep.tile([P, 4, 256], U8, name=f"w_perm{k}{q}", align_bytes=64)
+                w_perm[k, q] = wp
+                nc.vector.tensor_copy(
+                    out=wp[:].rearrange("p t (m b) -> p t m b", b=2),
+                    in_=w_raw[q][:, k, :].rearrange("p (m t b) -> p t m b", t=4, b=2),
+                )
+
+        def permute_wsc(q):
+            nc.vector.tensor_copy(
+                out=wsc[q][:],
+                in_=wsc_raw[:, :, HALF * q : HALF * (q + 1)].rearrange("p k (m t) -> p k t m", t=4),
+            )
+
+        th, z_il, z_codes, z_planes = {}, {}, {}, {}
+        h_ps = {}
+
+        def multiply_w(h, q, t):
+            ps = psum.tile([P, HALF], F32, name="mm", bufs=5)
+            h_ps[h, q, t] = ps
+            for k in range(2):
+                nc.tensor.matmul_mx(
+                    out=ps[:],
+                    lhsT=w_perm[k, q][:, t, :].bitcast(E2M1X4),
+                    lhsT_scale=wsc[q][:, k, t, :],
+                    rhs=x_codes[h, k][:].bitcast(E4M3X4),
+                    rhs_scale=x_planes[h, k][:],
+                    start=(k == 0),
+                    stop=(k == 1),
+                )
+
+        def tanh_h(h, q, t):
+            if t == 0:
+                th_hq = work.tile([P, 4, HALF], F32, name="th", bufs=3, align_bytes=64)
+                th[h, q] = th_hq
+            nc.scalar.activation(
+                out=th[h, q][:, t, :], in_=h_ps[h, q, t][:], func=ACT.Tanh, bias=c_col[:, q, t : t + 1]
+            )
+
+        def gain_z(h, q):
+            zi = work.tile([P, HALF, 4], BF16, name="z_il", bufs=3, align_bytes=64)
+            z_il[h, q] = zi
+            nc.vector.tensor_tensor(
+                out=zi[:].rearrange("p (m i) t -> p m t i", i=4),
+                in0=th[h, q][:].rearrange("p t (m i) -> p m t i", i=4),
+                in1=g_col[:, q, :].unsqueeze(1).unsqueeze(3).to_broadcast([P, HALF // 4, 4, 4]),
+                op=ALU.mult,
+            )
+
+        def quant_z(h, q):
+            zc = keep.tile([P, HALF], U32, name=f"z_codes{q}{h}", align_bytes=64)
+            zp = keep.tile([P, HALF], U8, name=f"z_planes{q}{h}", align_bytes=64)
+            z_codes[q, h], z_planes[q, h] = zc, zp
+            nc.vector.quantize_mx(
+                out=zc[:].bitcast(E4M3X4), scales=zp[:], in_=z_il[h, q][:].rearrange("p n t -> p (n t)")
+            )
+
+        half_pi = keep.tile([P, 1], F32, name="half_pi")
+        s_f = keep.tile([P, P], F32, name="s_f")
+        s_col = keep.tile([P, 8], F32, name="s_col")
+        s_turn = keep.tile([P, 8], F32, name="s_turn")
+        s_mean = keep.tile([P, 8], F32, name="s_mean")
+        s_nmean = keep.tile([P, 8], F32, name="s_nmean")
+        s_sq = keep.tile([P, 8], F32, name="s_sq")
+        th_q = keep.tile([P, 8], F32, name="th_q")
+        num = keep.tile([P, 8], F32, name="num")
+        den = keep.tile([P, 8], F32, name="den")
+        s_psi4 = keep.tile([P, 8], F32, name="s_psi4")
+
+        def prepare_s():
+            nc.gpsimd.tensor_scalar(half_pi[:], warm[:], math.pi / 2, None, ALU.add)
+            nc.gpsimd.tensor_copy(out=s_f[:], in_=s_rows[:])
+            s_ps = psum.tile([P, P], F32, name="tp", bufs=3)
+            nc.tensor.transpose(s_ps[:], s_f[:], ident[:])
+            nc.vector.tensor_copy(out=s_col[:], in_=s_ps[:, 0:8])
+            nc.gpsimd.tensor_tensor(s_sq[:], s_col[:], s_col[:], ALU.mult)
+            nc.gpsimd.tensor_scalar(s_turn[:], s_col[:], 1.0 / TWO_PI, None, ALU.mult)
+            nc.gpsimd.tensor_scalar(s_mean[:], s_col[:], 4.0 / N, None, ALU.mult)
+            nc.gpsimd.tensor_scalar(s_nmean[:], s_col[:], -4.0 / N, None, ALU.mult)
+
+        def prepare_psi():
+            nc.scalar.activation(out=th_q[:], in_=s_sq[:], func=ACT.Tanh, scale=0.25)
+            nc.vector.tensor_scalar(den[:], th_q[:], 1.0, None, ALU.add)
+            nc.vector.tensor_scalar(num[:], th_q[:], -1.0, 1.0, ALU.mult, ALU.add)
+            nc.vector.reciprocal(den[:], den[:])
+            nc.gpsimd.tensor_tensor(num[:], num[:], s_col[:], ALU.mult)
+            nc.gpsimd.tensor_tensor(num[:], num[:], den[:], ALU.mult)
+            nc.gpsimd.tensor_scalar(s_psi4[:], num[:], 4.0, None, ALU.mult)
+
+        out_view = out.rearrange("(b p) m -> p b m", p=P)
+        u_ps, turn_t, r_t, sin_t, cos_t, sin_sum, cos_sum = {}, {}, {}, {}, {}, {}, {}
+        abs_t, sin_s, cos_s, o_ps, o_sb = {}, {}, {}, {}, {}
+
+        def multiply_a(j, h):
+            ps = psum.tile([P, HALF], F32, name="mm", bufs=5)
+            u_ps[j, h] = ps
+            for q in range(2):
+                nc.tensor.matmul_mx(
+                    out=ps[:],
+                    lhsT=a_raw[:, q, 256 * j : 256 * (j + 1)].bitcast(E2M1X4),
+                    lhsT_scale=asc[:, q, P * j : P * (j + 1)],
+                    rhs=z_codes[q, h][:].bitcast(E4M3X4),
+                    rhs_scale=z_planes[q, h][:],
+                    start=(q == 0),
+                    stop=(q == 1),
+                )
+
+        def count_turns(j, h):
+            tt = work.tile([P, HALF], I32, name="turns", bufs=5)
+            turn_t[j, h] = tt
+            nc.vector.tensor_scalar(tt[:], u_ps[j, h][:], s_turn[:, j : j + 1], None, ALU.mult)
+
+        def take_turns(j, h):
+            if h == 0:
+                rr = work.tile([P, N], F32, name="r", bufs=5)
+                r_t[j] = rr
+            nc.vector.scalar_tensor_tensor(
+                out=r_t[j][:, HALF * h : HALF * (h + 1)],
+                in0=u_ps[j, h][:],
+                scalar=s_turn[:, j : j + 1],
+                in1=turn_t[j, h][:],
+                op0=ALU.mult,
+                op1=ALU.subtract,
+            )
+
+        def trig(j, parts):
+            if parts[0][0] == 0:
+                ra = work.tile([P, N], F32, name="r_abs", bufs=2)
+                su = work.tile([P, N], F32, name="sin_u", bufs=6)
+                cu = work.tile([P, N], F32, name="cos_u", bufs=6)
+                abs_t[j], sin_t[j], cos_t[j], sin_sum[j], cos_sum[j] = ra, su, cu, [], []
+            for lo, hi in parts:
+                ss = work.tile([P, 1], F32, name="sin_sum", bufs=8)
+                cs = work.tile([P, 1], F32, name="cos_sum", bufs=8)
+                sin_sum[j].append(ss)
+                cos_sum[j].append(cs)
+                nc.scalar.activation(out=abs_t[j][:, lo:hi], in_=r_t[j][:, lo:hi], func=ACT.Abs)
+                nc.scalar.activation(
+                    out=sin_t[j][:, lo:hi], in_=r_t[j][:, lo:hi], func=ACT.Sin, scale=TWO_PI, accum_out=ss[:]
+                )
+                nc.scalar.activation(
+                    out=cos_t[j][:, lo:hi],
+                    in_=abs_t[j][:, lo:hi],
+                    func=ACT.Sin,
+                    scale=-TWO_PI,
+                    bias=half_pi[:],
+                    accum_out=cs[:],
+                )
+
+        cos_k, sin_k = {}, {}
+
+        def weights(j):
+            ck = work.tile([P, 1], F32, name="cos_k", bufs=3)
+            sk = work.tile([P, 1], F32, name="sin_k", bufs=3)
+            cos_k[j], sin_k[j] = ck, sk
+            ss, cs = sin_sum[j], cos_sum[j]
+            if len(ss) == 2:
+                nc.vector.tensor_scalar(ck[:], ss[0][:], ss[1][:], s_mean[:, j : j + 1], ALU.add, ALU.mult)
+                both = work.tile([P, 1], F32, name="both", bufs=3)
+                nc.vector.tensor_scalar(both[:], cs[0][:], cs[1][:], None, ALU.add)
+            else:
+                nc.vector.tensor_scalar(ck[:], ss[0][:], s_mean[:, j : j + 1], None, ALU.mult)
+                both = cs[0]
+            nc.vector.tensor_scalar(
+                sk[:], both[:], s_nmean[:, j : j + 1], s_psi4[:, j : j + 1], ALU.mult, ALU.add
+            )
+
+        diag_t = {}
+
+        def weigh(j, cos_on):
+            ck, sk = cos_k[j], sin_k[j]
+            if cos_on == "pe":
+                dg = work.tile([P, P], F32, name="diag", bufs=2)
+                diag_t[j] = dg
+                nc.gpsimd.tensor_scalar(dg[:], ident[:], ck[:], 0.0, ALU.mult, ALU.add)
+            else:
+                co = work.tile([P, N], F32, name="cos_s", bufs=2)
+                cos_s[j] = co
+                if cos_on == "v":
+                    nc.vector.tensor_scalar(co[:], cos_t[j][:], ck[:], None, ALU.mult)
+                else:
+                    nc.gpsimd.tensor_scalar(co[:], cos_t[j][:], ck[:], 0.0, ALU.mult, ALU.add)
+            si = work.tile([P, N], F32, name="sin_s", bufs=2)
+            sin_s[j] = si
+            if cos_on == "v" and j == 7:
+                nc.vector.tensor_scalar(si[:], sin_t[j][:], sk[:], None, ALU.mult)
+            else:
+                nc.gpsimd.tensor_scalar(si[:], sin_t[j][:], sk[:], 0.0, ALU.mult, ALU.add)
+
+        def turn_out(j, hb):
+            ps = psum.tile([P, 4, P], F32, name="tp", bufs=3)
+            o_ps[j, hb] = ps
+            for b in range(4):
+                blk = slice(P * (4 * hb + b), P * (4 * hb + b + 1))
+                if j in diag_t:
+                    nc.tensor.matmul(ps[:, b, :], lhsT=cos_t[j][:, blk], rhs=diag_t[j][:], start=True, stop=False)
+                else:
+                    nc.tensor.matmul(
+                        ps[:, b, :], lhsT=cos_s[j][:, blk], rhs=ident[:], is_transpose=True, start=True, stop=False
+                    )
+                nc.tensor.matmul(
+                    ps[:, b, :], lhsT=sin_s[j][:, blk], rhs=ident[:], is_transpose=True, start=False, stop=True
+                )
+
+        def leave(j, hb, on_scalar=False):
+            if hb == 0:
+                ob = work.tile([P, 8, P], F32, name="o_sb", bufs=3)
+                o_sb[j] = ob
+            dst = o_sb[j][:, 4 * hb : 4 * hb + 4, :]
+            if on_scalar:
+                nc.scalar.copy(out=dst, in_=o_ps[j, hb][:])
+            else:
+                nc.vector.tensor_copy(out=dst, in_=o_ps[j, hb][:])
+            nc.sync.dma_start(
+                out=out_view[:, 4 * hb : 4 * hb + 4, P * j : P * (j + 1)], in_=dst
+            )
+
+        E = 0
+        LAG_T, LAG_L = 2, 3
+        COS = ["g","g","g","g","g","g","g","v"]
+
+        def s1(h, q):
+            for t in range(4):
+                multiply_w(h, q, t)
+                tanh_h(h, q, t)
+
+        def r_half(j, h):
+            multiply_a(j, h)
+            count_turns(j, h)
+            take_turns(j, h)
+
+        permute_w(0)
+        widen_x(0, True)
+        widen_x(3, False)
+        turn_x(0)
+        widen_x(1, True)
+        turn_x(1)
+        widen_x(2, True)
+        permute_wsc(0)
+        for k in range(2):
+            scale_x(0, k)
+        for k in range(2):
+            scale_x(1, k)
+        turn_x(3)
+        turn_x(2)
+        for k in range(2):
+            scale_x(3, k)
+        prepare_s()
+        for k in range(2):
+            scale_x(2, k)
+        for k in range(2):
+            quant_x(0, k)
+        for i in range(4, 7):
+            widen_x(i, True)
+        turn_x(4)
+        turn_x(5)
+        permute_w(1)
+        permute_wsc(1)
+        s1(0, 0)
+        for i in range(4, 6):
+            for k in range(2):
+                scale_x(i, k)
+        widen_x(7, False)
+        turn_x(6)
+        turn_x(7)
+        for i in range(6, 8):
+            for k in range(2):
+                scale_x(i, k)
+        s1(0, 1)
+        for k in range(2):
+            quant_x(1, k)
+        prepare_psi()
+        gain_z(0, 0)
+        s1(1, 0)
+        gain_z(0, 1)
+        quant_z(0, 0)
+        s1(1, 1)
+        quant_z(0, 1)
+        gain_z(1, 0)
+        quant_z(1, 0)
+        gain_z(1, 1)
+        quant_z(1, 1)
+        LEAVE_S = ((7, 1),)
+
+        def parts(j):
+            return [1] if j < E else [0, 1]
+
+        for h in parts(0):
+            multiply_a(0, h)
+        for j in range(8 + LAG_L):
+            if j + 1 < 8:
+                for h in parts(j + 1):
+                    multiply_a(j + 1, h)
+            if LAG_T <= j < 8 + LAG_T:
+                weights(j - LAG_T)
+                weigh(j - LAG_T, COS[j - LAG_T])
+            if j < 8:
+                for h in parts(j):
+                    count_turns(j, h)
+                if j >= LAG_L:
+                    leave(j - LAG_L, 0, (j - LAG_L, 0) in LEAVE_S)
+                for h in parts(j):
+                    take_turns(j, h)
+                trig(j, [(HALF, N)] if j < E else [(0, N)])
+            elif j >= LAG_L:
+                leave(j - LAG_L, 0, (j - LAG_L, 0) in LEAVE_S)
+            if j >= LAG_L:
+                leave(j - LAG_L, 1, (j - LAG_L, 1) in LEAVE_S)
+            if LAG_T <= j < 8 + LAG_T:
+                for hb in range(2):
+                    turn_out(j - LAG_T, hb)

@@ -95,11 +95,6 @@ def tile_lejepasigregrandomknotslicegrad_d2p_kernel(
         nc.sync.dma_start(out=a_raw[:].bitcast(I32), in_=a_words.rearrange("k p b -> p k b").bitcast(I32))
         load_scales(asc, a_scales)
 
-        xsc = keep.tile([P, 8, 2], F32, name="xsc")
-        xs_view = xs_all[:].rearrange("p (i k q) -> p i k q", i=8, k=2)
-        for quad in range(4):
-            rows = slice(32 * quad, 32 * quad + 32)
-            nc.gpsimd.tensor_copy(out=xsc[rows], in_=xs_view[rows, :, :, quad])
         c_col = keep.tile([P, 2, 4], F32, name="c_col")
         g_col = keep.tile([P, 2, 4], F32, name="g_col")
         nc.gpsimd.tensor_copy(out=c_col[:], in_=c_b[:])
@@ -107,20 +102,27 @@ def tile_lejepasigregrandomknotslicegrad_d2p_kernel(
 
         x_il, x_codes, x_planes = {}, {}, {}
         for h in range(2):
+            xi = keep.tile([P, 2, HALF, 4], BF16, name=f"x_il{h}", align_bytes=64)
+            x_il[h] = xi
             for k in range(2):
-                xi = keep.tile([P, HALF, 4], BF16, name=f"x_il{h}{k}", align_bytes=64)
                 xc = keep.tile([P, HALF], U32, name=f"x_codes{h}{k}", align_bytes=64)
                 xp = keep.tile([P, HALF], U8, name=f"x_planes{h}{k}", align_bytes=64)
-                x_il[h, k], x_codes[h, k], x_planes[h, k] = xi, xc, xp
+                x_codes[h, k], x_planes[h, k] = xc, xp
         x_bf, x_t = {}, {}
 
         def widen_x(i, on_scalar):
             wide = work.tile([P, F], BF16, name="x_bf", bufs=6, align_bytes=64)
             x_bf[i] = wide
-            if on_scalar:
-                nc.scalar.copy(out=wide[:], in_=x_raw[i][:].bitcast(E4M3))
-            else:
-                nc.vector.tensor_copy(out=wide[:], in_=x_raw[i][:].bitcast(E4M3))
+            for b in range(8):
+                cols = slice(P * b, P * (b + 1))
+                src = x_raw[i][:, cols].bitcast(E4M3)
+                factor = xs_all[:, 8 * i + b : 8 * i + b + 1]
+                if on_scalar:
+                    nc.scalar.activation(out=wide[:, cols], in_=src, func=ACT.Copy, scale=factor)
+                else:
+                    nc.vector.tensor_scalar(
+                        out=wide[:, cols], in0=src, scalar1=factor, scalar2=None, op0=ALU.mult
+                    )
 
         def turn_x(i):
             words = x_bf[i][:].bitcast(F32)
@@ -130,20 +132,20 @@ def tile_lejepasigregrandomknotslicegrad_d2p_kernel(
                 for u in range(2):
                     nc.tensor.transpose(xt[:, k, u, :], words[:, 256 * k + u : 256 * (k + 1) : 2], ident[:])
 
-        def scale_x(i, k, on_scalar=False):
+        def empty_x(i, on_scalar=False):
             h, b = divmod(i, 4)
-            dst = x_il[h, k][:, P * b : P * (b + 1), :].rearrange("p n (u e) -> p n u e", e=2)
-            src = x_t[i][:, k].bitcast(BF16).rearrange("p u (n e) -> p n u e", e=2)
+            dst = x_il[h][:, :, P * b : P * (b + 1), :].bitcast(F32)
+            src = x_t[i][:].rearrange("p k u n -> p k n u")
             if on_scalar:
-                nc.scalar.activation(out=dst, in_=src, func=ACT.Copy, scale=xsc[:, i, k : k + 1])
+                nc.scalar.copy(out=dst, in_=src)
             else:
-                nc.vector.tensor_scalar(out=dst, in0=src, scalar1=xsc[:, i, k : k + 1], scalar2=None, op0=ALU.mult)
+                nc.vector.tensor_copy(out=dst, in_=src)
 
         def quant_x(h, k):
             nc.vector.quantize_mx(
                 out=x_codes[h, k][:].bitcast(E4M3X4),
                 scales=x_planes[h, k][:],
-                in_=x_il[h, k][:].rearrange("p n t -> p (n t)"),
+                in_=x_il[h][:, k].rearrange("p n t -> p (n t)"),
             )
 
         w_perm = {}
@@ -167,7 +169,7 @@ def tile_lejepasigregrandomknotslicegrad_d2p_kernel(
                 in_=wsc_raw[:, :, HALF * q : HALF * (q + 1)].rearrange("p k (m t) -> p k t m", t=4),
             )
 
-        th, z_il, z_codes, z_planes = {}, {}, {}, {}
+        th, z_gained, z_il, z_codes, z_planes = {}, {}, {}, {}, {}
         h_ps = {}
 
         def multiply_w(h, q, t):
@@ -192,14 +194,22 @@ def tile_lejepasigregrandomknotslicegrad_d2p_kernel(
                 out=th[h, q][:, t, :], in_=h_ps[h, q, t][:], func=ACT.Tanh, bias=c_col[:, q, t : t + 1]
             )
 
-        def gain_z(h, q):
+        def gain_z(h, q, t, on_scalar):
+            if t == 0:
+                zg = work.tile([P, 4, HALF], BF16, name="z_gained", bufs=3, align_bytes=64)
+                z_gained[h, q] = zg
+            dst, src, factor = z_gained[h, q][:, t, :], th[h, q][:, t, :], g_col[:, q, t : t + 1]
+            if on_scalar:
+                nc.scalar.activation(out=dst, in_=src, func=ACT.Copy, scale=factor)
+            else:
+                nc.vector.tensor_scalar(out=dst, in0=src, scalar1=factor, scalar2=None, op0=ALU.mult)
+
+        def weave_z(h, q):
             zi = work.tile([P, HALF, 4], BF16, name="z_il", bufs=3, align_bytes=64)
             z_il[h, q] = zi
-            nc.vector.tensor_tensor(
+            nc.vector.tensor_copy(
                 out=zi[:].rearrange("p (m i) t -> p m t i", i=4),
-                in0=th[h, q][:].rearrange("p t (m i) -> p m t i", i=4),
-                in1=g_col[:, q, :].unsqueeze(1).unsqueeze(3).to_broadcast([P, HALF // 4, 4, 4]),
-                op=ALU.mult,
+                in_=z_gained[h, q][:].rearrange("p t (m i) -> p m t i", i=4),
             )
 
         def quant_z(h, q):
@@ -278,47 +288,64 @@ def tile_lejepasigregrandomknotslicegrad_d2p_kernel(
                 op1=ALU.subtract,
             )
 
-        def trig(j, parts):
-            if parts[0][0] == 0:
+        def sine(j, lo, hi):
+            ss = work.tile([P, 1], F32, name="sin_sum", bufs=8)
+            sin_sum[j].append(ss)
+            nc.scalar.activation(
+                out=sin_t[j][:, lo:hi], in_=r_t[j][:, lo:hi], func=ACT.Sin, scale=TWO_PI, accum_out=ss[:]
+            )
+
+        def cosine(j, lo, hi):
+            cs = work.tile([P, 1], F32, name="cos_sum", bufs=8)
+            cos_sum[j].append(cs)
+            nc.scalar.activation(
+                out=cos_t[j][:, lo:hi],
+                in_=abs_t[j][:, lo:hi],
+                func=ACT.Sin,
+                scale=-TWO_PI,
+                bias=half_pi[:],
+                accum_out=cs[:],
+            )
+
+        def magnitude(j, lo, hi):
+            if lo == 0:
                 ra = work.tile([P, N], F32, name="r_abs", bufs=2)
-                su = work.tile([P, N], F32, name="sin_u", bufs=6)
-                cu = work.tile([P, N], F32, name="cos_u", bufs=6)
+                su = work.tile([P, N], F32, name="sin_u", bufs=5)
+                cu = work.tile([P, N], F32, name="cos_u", bufs=5)
                 abs_t[j], sin_t[j], cos_t[j], sin_sum[j], cos_sum[j] = ra, su, cu, [], []
+            nc.scalar.activation(out=abs_t[j][:, lo:hi], in_=r_t[j][:, lo:hi], func=ACT.Abs)
+
+        def trig(j, parts):
             for lo, hi in parts:
-                ss = work.tile([P, 1], F32, name="sin_sum", bufs=8)
-                cs = work.tile([P, 1], F32, name="cos_sum", bufs=8)
-                sin_sum[j].append(ss)
-                cos_sum[j].append(cs)
-                nc.scalar.activation(out=abs_t[j][:, lo:hi], in_=r_t[j][:, lo:hi], func=ACT.Abs)
-                nc.scalar.activation(
-                    out=sin_t[j][:, lo:hi], in_=r_t[j][:, lo:hi], func=ACT.Sin, scale=TWO_PI, accum_out=ss[:]
-                )
-                nc.scalar.activation(
-                    out=cos_t[j][:, lo:hi],
-                    in_=abs_t[j][:, lo:hi],
-                    func=ACT.Sin,
-                    scale=-TWO_PI,
-                    bias=half_pi[:],
-                    accum_out=cs[:],
-                )
+                magnitude(j, lo, hi)
+                sine(j, lo, hi)
+                cosine(j, lo, hi)
 
         cos_k, sin_k = {}, {}
 
+        def cos_weight(j):
+            ck = warm[:]
+            for n, ss in enumerate(sin_sum[j]):
+                nxt = work.tile([P, 1], F32, name="cos_k", bufs=6)
+                nc.scalar.activation(
+                    out=nxt[:], in_=ss[:], func=ACT.Identity, scale=s_mean[:, j : j + 1], bias=ck
+                )
+                ck = nxt[:]
+            cos_k[j] = ck
+
+        def sin_weight(j):
+            sk = s_psi4[:, j : j + 1]
+            for n, cs in enumerate(cos_sum[j]):
+                nxt = work.tile([P, 1], F32, name="sin_k", bufs=6)
+                nc.scalar.activation(
+                    out=nxt[:], in_=cs[:], func=ACT.Identity, scale=s_nmean[:, j : j + 1], bias=sk
+                )
+                sk = nxt[:]
+            sin_k[j] = sk
+
         def weights(j):
-            ck = work.tile([P, 1], F32, name="cos_k", bufs=3)
-            sk = work.tile([P, 1], F32, name="sin_k", bufs=3)
-            cos_k[j], sin_k[j] = ck, sk
-            ss, cs = sin_sum[j], cos_sum[j]
-            if len(ss) == 2:
-                nc.vector.tensor_scalar(ck[:], ss[0][:], ss[1][:], s_mean[:, j : j + 1], ALU.add, ALU.mult)
-                both = work.tile([P, 1], F32, name="both", bufs=3)
-                nc.vector.tensor_scalar(both[:], cs[0][:], cs[1][:], None, ALU.add)
-            else:
-                nc.vector.tensor_scalar(ck[:], ss[0][:], s_mean[:, j : j + 1], None, ALU.mult)
-                both = cs[0]
-            nc.vector.tensor_scalar(
-                sk[:], both[:], s_nmean[:, j : j + 1], s_psi4[:, j : j + 1], ALU.mult, ALU.add
-            )
+            cos_weight(j)
+            sin_weight(j)
 
         diag_t = {}
 
@@ -327,20 +354,26 @@ def tile_lejepasigregrandomknotslicegrad_d2p_kernel(
             if cos_on == "pe":
                 dg = work.tile([P, P], F32, name="diag", bufs=2)
                 diag_t[j] = dg
-                nc.gpsimd.tensor_scalar(dg[:], ident[:], ck[:], 0.0, ALU.mult, ALU.add)
+                nc.gpsimd.tensor_scalar(dg[:], ident[:], ck, 0.0, ALU.mult, ALU.add)
             else:
                 co = work.tile([P, N], F32, name="cos_s", bufs=2)
                 cos_s[j] = co
                 if cos_on == "v":
-                    nc.vector.tensor_scalar(co[:], cos_t[j][:], ck[:], None, ALU.mult)
+                    nc.vector.tensor_scalar(co[:], cos_t[j][:], ck, None, ALU.mult)
                 else:
-                    nc.gpsimd.tensor_scalar(co[:], cos_t[j][:], ck[:], 0.0, ALU.mult, ALU.add)
+                    nc.gpsimd.tensor_scalar(co[:], cos_t[j][:], ck, 0.0, ALU.mult, ALU.add)
             si = work.tile([P, N], F32, name="sin_s", bufs=2)
             sin_s[j] = si
-            if cos_on == "v" and j == 7:
-                nc.vector.tensor_scalar(si[:], sin_t[j][:], sk[:], None, ALU.mult)
-            else:
-                nc.gpsimd.tensor_scalar(si[:], sin_t[j][:], sk[:], 0.0, ALU.mult, ALU.add)
+            nc.gpsimd.tensor_scalar(si[:], sin_t[j][:], sk, 0.0, ALU.mult, ALU.add)
+
+        def weigh_on_vector(j, lo, hi):
+            nc.vector.tensor_scalar(cos_s[j][:, lo:hi], cos_t[j][:, lo:hi], cos_k[j], None, ALU.mult)
+            nc.vector.tensor_scalar(sin_s[j][:, lo:hi], sin_t[j][:, lo:hi], sin_k[j], None, ALU.mult)
+
+        def weighed_tiles(j):
+            co = work.tile([P, N], F32, name="cos_s", bufs=2)
+            si = work.tile([P, N], F32, name="sin_s", bufs=2)
+            cos_s[j], sin_s[j] = co, si
 
         def turn_out(j, hb):
             ps = psum.tile([P, 4, P], F32, name="tp", bufs=3)
@@ -370,97 +403,140 @@ def tile_lejepasigregrandomknotslicegrad_d2p_kernel(
                 out=out_view[:, 4 * hb : 4 * hb + 4, P * j : P * (j + 1)], in_=dst
             )
 
-        E = 0
+        E = 2
         LAG_T, LAG_L = 2, 3
         COS = ["g","g","g","g","g","g","g","v"]
+        LEAVE_S = ()
+        SEQ = [0,1,2,3,4,5,6,7]
+        WIDE_V = [3, 6]
+        GAIN_S = {(0, 0): (), (0, 1): (), (1, 0): (), (1, 1): (0, 1)}
+        EMPTY_S = [7]
 
         def s1(h, q):
             for t in range(4):
                 multiply_w(h, q, t)
                 tanh_h(h, q, t)
 
-        def r_half(j, h):
-            multiply_a(j, h)
-            count_turns(j, h)
-            take_turns(j, h)
+        def gain(h, q, on_scalar):
+            for t in range(4):
+                if (t in GAIN_S[h, q]) == on_scalar:
+                    gain_z(h, q, t, on_scalar)
+
+        def early(js):
+            for j in js:
+                count_turns(j, 0)
+            for j in js:
+                take_turns(j, 0)
+                trig(j, [(0, HALF)])
 
         permute_w(0)
-        widen_x(0, True)
-        widen_x(3, False)
-        turn_x(0)
-        widen_x(1, True)
-        turn_x(1)
-        widen_x(2, True)
+        for i in range(3):
+            widen_x(i, i not in WIDE_V)
+            turn_x(i)
         permute_wsc(0)
-        for k in range(2):
-            scale_x(0, k)
-        for k in range(2):
-            scale_x(1, k)
+        empty_x(0, 0 in EMPTY_S)
+        widen_x(3, 3 not in WIDE_V)
+        empty_x(1, 1 in EMPTY_S)
         turn_x(3)
-        turn_x(2)
-        for k in range(2):
-            scale_x(3, k)
-        prepare_s()
-        for k in range(2):
-            scale_x(2, k)
+        empty_x(2, 2 in EMPTY_S)
+        empty_x(3, 3 in EMPTY_S)
         for k in range(2):
             quant_x(0, k)
-        for i in range(4, 7):
-            widen_x(i, True)
-        turn_x(4)
-        turn_x(5)
-        permute_w(1)
-        permute_wsc(1)
-        s1(0, 0)
         for i in range(4, 6):
-            for k in range(2):
-                scale_x(i, k)
-        widen_x(7, False)
-        turn_x(6)
-        turn_x(7)
+            widen_x(i, i not in WIDE_V)
+            turn_x(i)
+        permute_w(1)
+        s1(0, 0)
+        permute_wsc(1)
+        prepare_s()
+        empty_x(4, 4 in EMPTY_S)
         for i in range(6, 8):
-            for k in range(2):
-                scale_x(i, k)
+            widen_x(i, i not in WIDE_V)
+        turn_x(6)
+        empty_x(5, 5 in EMPTY_S)
+        turn_x(7)
+        empty_x(6, 6 in EMPTY_S)
+        empty_x(7, 7 in EMPTY_S)
         s1(0, 1)
+        gain(0, 0, True)
+        gain(0, 0, False)
         for k in range(2):
             quant_x(1, k)
-        prepare_psi()
-        gain_z(0, 0)
+        weave_z(0, 0)
         s1(1, 0)
-        gain_z(0, 1)
+        gain(0, 1, True)
+        gain(0, 1, False)
         quant_z(0, 0)
+        weave_z(0, 1)
         s1(1, 1)
+        gain(1, 0, True)
+        gain(1, 0, False)
         quant_z(0, 1)
-        gain_z(1, 0)
+        weave_z(1, 0)
+        prepare_psi()
+        for j in range(E):
+            multiply_a(j, 0)
+        gain(1, 1, True)
+        gain(1, 1, False)
         quant_z(1, 0)
-        gain_z(1, 1)
+        early(range(min(E, 2)))
+        weave_z(1, 1)
+        if E > 2:
+            early(range(2, E))
         quant_z(1, 1)
-        LEAVE_S = ((7, 1),)
 
         def parts(j):
             return [1] if j < E else [0, 1]
 
-        for h in parts(0):
-            multiply_a(0, h)
-        for j in range(8 + LAG_L):
-            if j + 1 < 8:
-                for h in parts(j + 1):
-                    multiply_a(j + 1, h)
-            if LAG_T <= j < 8 + LAG_T:
-                weights(j - LAG_T)
-                weigh(j - LAG_T, COS[j - LAG_T])
-            if j < 8:
-                for h in parts(j):
-                    count_turns(j, h)
-                if j >= LAG_L:
-                    leave(j - LAG_L, 0, (j - LAG_L, 0) in LEAVE_S)
-                for h in parts(j):
-                    take_turns(j, h)
+        for h in parts(SEQ[0]):
+            multiply_a(SEQ[0], h)
+        for i in range(8):
+            j = SEQ[i]
+            if i + 1 < 8:
+                for h in parts(SEQ[i + 1]):
+                    multiply_a(SEQ[i + 1], h)
+            w = SEQ[i - LAG_T] if i >= LAG_T else None
+            v = SEQ[i - LAG_L] if i >= LAG_L else None
+            for h in parts(j):
+                count_turns(j, h)
+            if len(parts(j)) == 1 and v is not None:
+                leave(v, 0, (v, 0) in LEAVE_S)
+            for h in parts(j):
+                take_turns(j, h)
+            if i < 7:
                 trig(j, [(HALF, N)] if j < E else [(0, N)])
-            elif j >= LAG_L:
-                leave(j - LAG_L, 0, (j - LAG_L, 0) in LEAVE_S)
-            if j >= LAG_L:
-                leave(j - LAG_L, 1, (j - LAG_L, 1) in LEAVE_S)
-            if LAG_T <= j < 8 + LAG_T:
+                weights(j)
+                if i < 6:
+                    weigh(j, COS[j])
+            if len(parts(j)) == 2 and v is not None:
+                leave(v, 0, (v, 0) in LEAVE_S)
+            if v is not None:
+                leave(v, 1, (v, 1) in LEAVE_S)
+            if w is not None:
                 for hb in range(2):
-                    turn_out(j - LAG_T, hb)
+                    turn_out(w, hb)
+        j, w = SEQ[7], SEQ[6]
+        magnitude(j, 0, N)
+        sine(j, 0, N)
+        cos_weight(j)
+        for lo in (0, HALF):
+            cosine(j, lo, lo + HALF)
+        sin_weight(j)
+        for v in range(8 - LAG_T, 6):
+            for hb in range(2):
+                turn_out(SEQ[v], hb)
+        weighed_tiles(w)
+        weigh_on_vector(w, 0, N)
+        for hb in range(2):
+            turn_out(w, hb)
+        for v in range(8 - LAG_L, 6):
+            for hb in range(2):
+                leave(SEQ[v], hb, (SEQ[v], hb) in LEAVE_S)
+        weighed_tiles(j)
+        leave(w, 0, False)
+        for hb in range(2):
+            weigh_on_vector(j, HALF * hb, HALF * (hb + 1))
+            turn_out(j, hb)
+        leave(w, 1, True)
+        leave(j, 0, True)
+        leave(j, 1, False)

@@ -95,6 +95,11 @@ def tile_lejepasigregrandomknotslicegrad_d2p_kernel(
         nc.sync.dma_start(out=a_raw[:].bitcast(I32), in_=a_words.rearrange("k p b -> p k b").bitcast(I32))
         load_scales(asc, a_scales)
 
+        xsc = keep.tile([P, 8, 2], F32, name="xsc")
+        xs_view = xs_all[:].rearrange("p (i k q) -> p i k q", i=8, k=2)
+        for quad in range(4):
+            rows = slice(32 * quad, 32 * quad + 32)
+            nc.gpsimd.tensor_copy(out=xsc[rows], in_=xs_view[rows, :, :, quad])
         c_col = keep.tile([P, 2, 4], F32, name="c_col")
         g_col = keep.tile([P, 2, 4], F32, name="g_col")
         nc.gpsimd.tensor_copy(out=c_col[:], in_=c_b[:])
@@ -113,16 +118,10 @@ def tile_lejepasigregrandomknotslicegrad_d2p_kernel(
         def widen_x(i, on_scalar):
             wide = work.tile([P, F], BF16, name="x_bf", bufs=6, align_bytes=64)
             x_bf[i] = wide
-            for b in range(8):
-                cols = slice(P * b, P * (b + 1))
-                src = x_raw[i][:, cols].bitcast(E4M3)
-                factor = xs_all[:, 8 * i + b : 8 * i + b + 1]
-                if on_scalar:
-                    nc.scalar.activation(out=wide[:, cols], in_=src, func=ACT.Copy, scale=factor)
-                else:
-                    nc.vector.tensor_scalar(
-                        out=wide[:, cols], in0=src, scalar1=factor, scalar2=None, op0=ALU.mult
-                    )
+            if on_scalar:
+                nc.scalar.copy(out=wide[:], in_=x_raw[i][:].bitcast(E4M3))
+            else:
+                nc.vector.tensor_copy(out=wide[:], in_=x_raw[i][:].bitcast(E4M3))
 
         def turn_x(i):
             words = x_bf[i][:].bitcast(F32)
@@ -134,12 +133,15 @@ def tile_lejepasigregrandomknotslicegrad_d2p_kernel(
 
         def empty_x(i, on_scalar=False):
             h, b = divmod(i, 4)
-            dst = x_il[h][:, :, P * b : P * (b + 1), :].bitcast(F32)
-            src = x_t[i][:].rearrange("p k u n -> p k n u")
-            if on_scalar:
-                nc.scalar.copy(out=dst, in_=src)
-            else:
-                nc.vector.tensor_copy(out=dst, in_=src)
+            for k in range(2):
+                dst = x_il[h][:, k, P * b : P * (b + 1), :].rearrange("p n (u e) -> p n u e", e=2)
+                src = x_t[i][:, k].bitcast(BF16).rearrange("p u (n e) -> p n u e", e=2)
+                if on_scalar:
+                    nc.scalar.activation(out=dst, in_=src, func=ACT.Copy, scale=xsc[:, i, k : k + 1])
+                else:
+                    nc.vector.tensor_scalar(
+                        out=dst, in0=src, scalar1=xsc[:, i, k : k + 1], scalar2=None, op0=ALU.mult
+                    )
 
         def quant_x(h, k):
             nc.vector.quantize_mx(
@@ -405,10 +407,10 @@ def tile_lejepasigregrandomknotslicegrad_d2p_kernel(
 
         E = 2
         LAG_T, LAG_L = 2, 3
-        COS = ["g","g","g","g","g","g","g","v"]
+        COS = ["pe","g","pe","g","pe","g","g","v"]
         LEAVE_S = ()
         SEQ = [0,1,2,3,4,5,6,7]
-        WIDE_V = [3, 6]
+        WIDE_V = [6]
         GAIN_S = {(0, 0): (), (0, 1): (), (1, 0): (), (1, 1): (0, 1)}
         EMPTY_S = [7]
 

@@ -222,6 +222,17 @@ def tile_lejepasigregrandomknotslicegrad_d2p_kernel(
                 out=zc[:].bitcast(E4M3X4), scales=zp[:], in_=z_il[h, q][:].rearrange("p n t -> p (n t)")
             )
 
+        def heat(n):
+            for i in range(n):
+                ps = psum.tile([P, P], F32, name="mm", bufs=5)
+                nc.tensor.matmul(ps[:], lhsT=ident[:], rhs=ident[:], start=True, stop=True)
+
+        def heat_on(h, q, n):
+            for t in range(n):
+                ps = psum.tile([P, HALF], F32, name="mm", bufs=5)
+                src = z_gained[h, q]
+                nc.tensor.matmul(ps[:], lhsT=src[:, t, 0:P], rhs=src[:, t, :], start=True, stop=True)
+
         half_pi = keep.tile([P, 1], F32, name="half_pi")
         s_f = keep.tile([P, P], F32, name="s_f")
         s_col = keep.tile([P, 8], F32, name="s_col")
@@ -245,8 +256,10 @@ def tile_lejepasigregrandomknotslicegrad_d2p_kernel(
             nc.gpsimd.tensor_scalar(s_mean[:], s_col[:], 4.0 / N, None, ALU.mult)
             nc.gpsimd.tensor_scalar(s_nmean[:], s_col[:], -4.0 / N, None, ALU.mult)
 
-        def prepare_psi():
+        def start_psi():
             nc.scalar.activation(out=th_q[:], in_=s_sq[:], func=ACT.Tanh, scale=0.25)
+
+        def prepare_psi():
             nc.vector.tensor_scalar(den[:], th_q[:], 1.0, None, ALU.add)
             nc.vector.tensor_scalar(num[:], th_q[:], -1.0, 1.0, ALU.mult, ALU.add)
             nc.vector.reciprocal(den[:], den[:])
@@ -326,14 +339,12 @@ def tile_lejepasigregrandomknotslicegrad_d2p_kernel(
         cos_k, sin_k = {}, {}
 
         def cos_weight(j):
-            ck = warm[:]
-            for n, ss in enumerate(sin_sum[j]):
-                nxt = work.tile([P, 1], F32, name="cos_k", bufs=6)
-                nc.scalar.activation(
-                    out=nxt[:], in_=ss[:], func=ACT.Identity, scale=s_mean[:, j : j + 1], bias=ck
-                )
-                ck = nxt[:]
-            cos_k[j] = ck
+            ck = sin_sum[j][0]
+            if len(sin_sum[j]) == 2:
+                both = work.tile([P, 1], F32, name="both", bufs=4)
+                nc.scalar.activation(out=both[:], in_=ck[:], func=ACT.Identity, bias=sin_sum[j][1][:])
+                ck = both
+            cos_k[j] = ck[:]
 
         def sin_weight(j):
             sk = s_psi4[:, j : j + 1]
@@ -356,20 +367,22 @@ def tile_lejepasigregrandomknotslicegrad_d2p_kernel(
             if cos_on == "pe":
                 dg = work.tile([P, P], F32, name="diag", bufs=2)
                 diag_t[j] = dg
-                nc.gpsimd.tensor_scalar(dg[:], ident[:], ck, 0.0, ALU.mult, ALU.add)
+                nc.gpsimd.tensor_scalar(dg[:], ident[:], ck, s_mean[:, j : j + 1], ALU.mult, ALU.mult)
             else:
                 co = work.tile([P, N], F32, name="cos_s", bufs=2)
                 cos_s[j] = co
                 if cos_on == "v":
-                    nc.vector.tensor_scalar(co[:], cos_t[j][:], ck, None, ALU.mult)
+                    nc.vector.tensor_scalar(co[:], cos_t[j][:], ck, s_mean[:, j : j + 1], ALU.mult, ALU.mult)
                 else:
-                    nc.gpsimd.tensor_scalar(co[:], cos_t[j][:], ck, 0.0, ALU.mult, ALU.add)
+                    nc.gpsimd.tensor_scalar(co[:], cos_t[j][:], ck, s_mean[:, j : j + 1], ALU.mult, ALU.mult)
             si = work.tile([P, N], F32, name="sin_s", bufs=2)
             sin_s[j] = si
             nc.gpsimd.tensor_scalar(si[:], sin_t[j][:], sk, 0.0, ALU.mult, ALU.add)
 
         def weigh_on_vector(j, lo, hi):
-            nc.vector.tensor_scalar(cos_s[j][:, lo:hi], cos_t[j][:, lo:hi], cos_k[j], None, ALU.mult)
+            nc.vector.tensor_scalar(
+                cos_s[j][:, lo:hi], cos_t[j][:, lo:hi], cos_k[j], s_mean[:, j : j + 1], ALU.mult, ALU.mult
+            )
             nc.vector.tensor_scalar(sin_s[j][:, lo:hi], sin_t[j][:, lo:hi], sin_k[j], None, ALU.mult)
 
         def weighed_tiles(j):
@@ -406,97 +419,102 @@ def tile_lejepasigregrandomknotslicegrad_d2p_kernel(
             )
 
         E = 2
-        LAG_T, LAG_L = 2, 3
-        COS = ["pe","g","pe","g","pe","g","g","v"]
+        LAG_T, LAG_L = 3, 4
+        COS = ["g","g","g","g","g","g","g","v"]
         LEAVE_S = ()
-        SEQ = [0,1,2,3,4,5,6,7]
-        WIDE_V = [6]
-        GAIN_S = {(0, 0): (), (0, 1): (), (1, 0): (), (1, 1): (0, 1)}
-        EMPTY_S = [7]
+        SEQ = [0, 2, 1, 3, 4, 5, 6, 7]
+        WIDE_V = [2, 3]
+        GAIN_S = {(0, 0): (), (0, 1): (), (1, 0): (), (1, 1): (1, 2, 3)}
+        EMPTY_S = [0, 1]
 
         def s1(h, q):
             for t in range(4):
                 multiply_w(h, q, t)
                 tanh_h(h, q, t)
 
-        def gain(h, q, on_scalar):
-            for t in range(4):
-                if (t in GAIN_S[h, q]) == on_scalar:
-                    gain_z(h, q, t, on_scalar)
-
-        def early(js):
-            for j in js:
-                count_turns(j, 0)
-            for j in js:
-                take_turns(j, 0)
-                trig(j, [(0, HALF)])
-
-        permute_w(0)
-        for i in range(3):
+        def widen(i):
             widen_x(i, i not in WIDE_V)
-            turn_x(i)
+
+        def empty(i):
+            empty_x(i, i in EMPTY_S)
+
+        def gain(h, q):
+            for t in range(4):
+                gain_z(h, q, t, t in GAIN_S[h, q])
+
+        heat(6)
+        permute_w(0)
+        widen(0)
+        widen(1)
+        turn_x(0)
+        heat(1)
+        empty(0)
+        widen(2)
+        turn_x(1)
+        heat(1)
         permute_wsc(0)
-        empty_x(0, 0 in EMPTY_S)
-        widen_x(3, 3 not in WIDE_V)
-        empty_x(1, 1 in EMPTY_S)
+        empty(1)
+        widen(3)
+        turn_x(2)
+        heat(1)
         turn_x(3)
-        empty_x(2, 2 in EMPTY_S)
-        empty_x(3, 3 in EMPTY_S)
+        heat(1)
+        empty(2)
+        empty(3)
         for k in range(2):
             quant_x(0, k)
-        for i in range(4, 6):
-            widen_x(i, i not in WIDE_V)
-            turn_x(i)
-        permute_w(1)
-        s1(0, 0)
-        permute_wsc(1)
         prepare_s()
-        empty_x(4, 4 in EMPTY_S)
-        for i in range(6, 8):
-            widen_x(i, i not in WIDE_V)
-        turn_x(6)
-        empty_x(5, 5 in EMPTY_S)
-        turn_x(7)
-        empty_x(6, 6 in EMPTY_S)
-        empty_x(7, 7 in EMPTY_S)
+        widen(4)
+        widen(5)
+        permute_w(1)
+        permute_wsc(1)
+        s1(0, 0)
+        turn_x(4)
+        turn_x(5)
+        empty(4)
+        empty(5)
+        widen(6)
+        widen(7)
         s1(0, 1)
-        gain(0, 0, True)
-        gain(0, 0, False)
+        start_psi()
+        turn_x(6)
+        turn_x(7)
+        gain(0, 0)
+        empty(6)
+        empty(7)
         for k in range(2):
             quant_x(1, k)
         weave_z(0, 0)
         s1(1, 0)
-        gain(0, 1, True)
-        gain(0, 1, False)
+        gain(0, 1)
+        prepare_psi()
         quant_z(0, 0)
         weave_z(0, 1)
         s1(1, 1)
-        gain(1, 0, True)
-        gain(1, 0, False)
+        gain(1, 0)
         quant_z(0, 1)
         weave_z(1, 0)
-        prepare_psi()
+        heat_on(1, 0, 2)
         for j in range(E):
             multiply_a(j, 0)
-        gain(1, 1, True)
-        gain(1, 1, False)
+        gain(1, 1)
+        for j in range(E):
+            count_turns(j, 0)
         quant_z(1, 0)
-        early(range(min(E, 2)))
+        for j in range(E):
+            take_turns(j, 0)
+            trig(j, [(0, HALF)])
         weave_z(1, 1)
-        if E > 2:
-            early(range(2, E))
         quant_z(1, 1)
 
         def parts(j):
             return [1] if j < E else [0, 1]
 
-        for h in parts(SEQ[0]):
-            multiply_a(SEQ[0], h)
+        coming = [(j, h) for j in SEQ for h in parts(j)]
+        for n in range(2):
+            multiply_a(*coming.pop(0))
         for i in range(8):
             j = SEQ[i]
-            if i + 1 < 8:
-                for h in parts(SEQ[i + 1]):
-                    multiply_a(SEQ[i + 1], h)
             w = SEQ[i - LAG_T] if i >= LAG_T else None
             v = SEQ[i - LAG_L] if i >= LAG_L else None
             for h in parts(j):
@@ -514,8 +532,11 @@ def tile_lejepasigregrandomknotslicegrad_d2p_kernel(
                 leave(v, 0, (v, 0) in LEAVE_S)
             if v is not None:
                 leave(v, 1, (v, 1) in LEAVE_S)
-            if w is not None:
-                for hb in range(2):
+            for hb in range(2):
+                if len(coming) > 0 and i >= 0:
+                    multiply_a(*coming.pop(0))
+                if w is not None:
+                    heat(2)
                     turn_out(w, hb)
         j, w = SEQ[7], SEQ[6]
         magnitude(j, 0, N)
@@ -526,10 +547,12 @@ def tile_lejepasigregrandomknotslicegrad_d2p_kernel(
         sin_weight(j)
         for v in range(8 - LAG_T, 6):
             for hb in range(2):
+                heat(2)
                 turn_out(SEQ[v], hb)
         weighed_tiles(w)
         weigh_on_vector(w, 0, N)
         for hb in range(2):
+            heat(2)
             turn_out(w, hb)
         for v in range(8 - LAG_L, 6):
             for hb in range(2):
@@ -537,6 +560,7 @@ def tile_lejepasigregrandomknotslicegrad_d2p_kernel(
         weighed_tiles(j)
         leave(w, 0, False)
         for hb in range(2):
+            heat(2)
             weigh_on_vector(j, HALF * hb, HALF * (hb + 1))
             turn_out(j, hb)
         leave(w, 1, True)

@@ -4,8 +4,8 @@ from contextlib import ExitStack
 import concourse.mybir as mybir
 from concourse.masks import make_identity
 
-N, F, D, M = 1024, 1024, 1024, 1024
-FLOPS = 2 * N * F * D + 2 * N * D * M
+ROWS, FEATURES, CHANNELS, SLICES = 1024, 1024, 1024, 1024
+FLOPS = 2 * ROWS * FEATURES * CHANNELS + 2 * ROWS * CHANNELS * SLICES
 
 F32 = mybir.dt.float32
 BF16 = mybir.dt.bfloat16
@@ -19,8 +19,20 @@ ALU = mybir.AluOpType
 ACT = mybir.ActivationFunctionType
 
 P = 128
+PACK = 4
+GROUP = P * PACK
+GROUPS = 2
 HALF = 512
+HALVES = ROWS // HALF
+ROW_TILES = ROWS // P
+HALF_TILES = HALF // P
+SLICE_TILES = SLICES // P
 TWO_PI = 2.0 * math.pi
+
+EARLY = 2
+TURN_LAG = 3
+LEAVE_LAG = 4
+VECTOR_TILES = 2
 
 
 def tile_lejepasigregrandomknotslicegrad_d2p_kernel(
@@ -33,536 +45,436 @@ def tile_lejepasigregrandomknotslicegrad_d2p_kernel(
         psum = ctx.enter_context(tc.psum_pool(name="psum", bufs=1))
         ctx.enter_context(tc.manual_schedule())
 
-        warm = keep.tile([P, 1], F32, name="warm")
-        warm_out = keep.tile([P, 1], F32, name="warm_out")
-        nc.vector.memset(warm[:], 0.0)
-        wsc_raw = keep.tile([P, 2, D], U8, name="wsc_raw", align_bytes=64)
-        asc = keep.tile([P, 2, M], U8, name="asc", align_bytes=64)
-        nc.vector.memset(wsc_raw[:].bitcast(I32), 0)
+        zero = keep.tile([P, 1], F32, name="zero")
+        silu_zero = keep.tile([P, 1], F32, name="silu_zero")
+        half_pi = keep.tile([P, 1], F32, name="half_pi")
+        ident = keep.tile([P, P], F32, name="ident")
+        nc.vector.memset(zero[:], 0.0)
+
+        w_scale_rows = keep.tile([P, GROUPS, CHANNELS], U8, name="w_scale_rows", align_bytes=64)
+        a_scale_tile = keep.tile([P, GROUPS, SLICES], U8, name="a_scale_tile", align_bytes=64)
+        nc.vector.memset(w_scale_rows[:].bitcast(I32), 0)
         s_rows = keep.tile([P, P], BF16, name="s_rows")
         nc.gpsimd.memset(s_rows[:], 0.0)
-        ident = keep.tile([P, P], F32, name="ident")
         make_identity(nc, ident[:])
-        nc.gpsimd.memset(asc[:].bitcast(I32), 0)
+        nc.gpsimd.memset(a_scale_tile[:].bitcast(I32), 0)
 
-        xs_all = keep.tile([P, 64], F32, name="xs_all")
-        nc.scalar.dma_start(out=xs_all[:], in_=x_scale.rearrange("i j -> (i j)").partition_broadcast(P))
-        nc.scalar.activation(out=warm_out[:], in_=warm[:], func=ACT.Silu)
-        c_b = keep.tile([P, 2, 4], BF16, name="c_b")
-        g_b = keep.tile([P, 2, 4], BF16, name="g_b")
-        nc.scalar.dma_start(out=s_rows[0:8, :], in_=s.rearrange("(j p) -> j p", p=P))
-        nc.scalar.dma_start(out=c_b[:], in_=c.rearrange("(q p t) -> p q t", p=P, t=4))
-        nc.scalar.dma_start(out=g_b[:], in_=g.rearrange("(q p t) -> p q t", p=P, t=4))
+        x_scale_all = keep.tile([P, ROW_TILES * 8], F32, name="x_scale_all")
+        c_words = keep.tile([P, GROUPS, PACK], BF16, name="c_words")
+        g_words = keep.tile([P, GROUPS, PACK], BF16, name="g_words")
+        nc.scalar.dma_start(out=x_scale_all[:], in_=x_scale.rearrange("i j -> (i j)").partition_broadcast(P))
+        nc.scalar.activation(out=silu_zero[:], in_=zero[:], func=ACT.Silu)
+        nc.scalar.dma_start(out=s_rows[0:SLICE_TILES, :], in_=s.rearrange("(j p) -> j p", p=P))
+        nc.scalar.dma_start(out=c_words[:], in_=c.rearrange("(q p t) -> p q t", p=P, t=PACK))
+        nc.scalar.dma_start(out=g_words[:], in_=g.rearrange("(q p t) -> p q t", p=P, t=PACK))
 
         x_raw = []
-        for i in range(8):
-            x_raw_i = keep.tile([P, F], U8, name=f"x_raw{i}", align_bytes=64)
+        for i in range(ROW_TILES):
+            x_raw_i = keep.tile([P, FEATURES], U8, name=f"x_raw{i}", align_bytes=64)
             x_raw.append(x_raw_i)
         w_raw = []
-        for q in range(2):
-            w_raw_q = keep.tile([P, 2, 1024], U8, name=f"w_raw{q}", align_bytes=64)
+        for q in range(GROUPS):
+            w_raw_q = keep.tile([P, GROUPS, 2 * GROUP], U8, name=f"w_raw{q}", align_bytes=64)
             w_raw.append(w_raw_q)
-        a_raw = keep.tile([P, 2, 2 * M], U8, name="a_raw", align_bytes=64)
+        a_codes = keep.tile([P, GROUPS, 2 * SLICES], U8, name="a_codes", align_bytes=64)
 
         def load_x(i):
             nc.sync.dma_start(out=x_raw[i][:], in_=x_bytes[P * i : P * (i + 1), :])
 
-        w_view = w_words.rearrange("k p b -> p k b")
-
         def load_w(q):
-            nc.sync.dma_start(
-                out=w_raw[q][:].bitcast(I32), in_=w_view[:, :, 1024 * q : 1024 * (q + 1)].bitcast(I32)
-            )
+            columns = w_words.rearrange("k p b -> p k b")[:, :, 2 * GROUP * q : 2 * GROUP * (q + 1)]
+            nc.sync.dma_start(out=w_raw[q][:].bitcast(I32), in_=columns.bitcast(I32))
 
-        def load_scales(tile, src):
-            for quad in range(4):
+        def load_scale_rows(tile, rows):
+            for quadrant in range(4):
                 nc.sync.dma_start(
-                    out=tile[32 * quad : 32 * quad + 4].bitcast(I32),
-                    in_=src[:, 4 * quad : 4 * quad + 4, :].rearrange("k r n -> r k n").bitcast(I32),
+                    out=tile[32 * quadrant : 32 * quadrant + 4].bitcast(I32),
+                    in_=rows[:, 4 * quadrant : 4 * quadrant + 4, :].rearrange("k r n -> r k n").bitcast(I32),
                 )
 
         load_w(0)
-        load_x(0)
-        load_x(1)
-        load_x(2)
-        load_scales(wsc_raw, w_scales)
+        for i in range(3):
+            load_x(i)
+        load_scale_rows(w_scale_rows, w_scales)
         load_x(3)
         load_x(4)
         load_w(1)
-        load_x(5)
-        load_x(6)
-        load_x(7)
-        nc.sync.dma_start(out=a_raw[:].bitcast(I32), in_=a_words.rearrange("k p b -> p k b").bitcast(I32))
-        load_scales(asc, a_scales)
+        for i in range(5, ROW_TILES):
+            load_x(i)
+        nc.sync.dma_start(out=a_codes[:].bitcast(I32), in_=a_words.rearrange("k p b -> p k b").bitcast(I32))
+        load_scale_rows(a_scale_tile, a_scales)
 
-        xsc = keep.tile([P, 8, 2], F32, name="xsc")
-        xs_view = xs_all[:].rearrange("p (i k q) -> p i k q", i=8, k=2)
-        for quad in range(4):
-            rows = slice(32 * quad, 32 * quad + 32)
-            nc.gpsimd.tensor_copy(out=xsc[rows], in_=xs_view[rows, :, :, quad])
-        c_col = keep.tile([P, 2, 4], F32, name="c_col")
-        g_col = keep.tile([P, 2, 4], F32, name="g_col")
-        nc.gpsimd.tensor_copy(out=c_col[:], in_=c_b[:])
-        nc.gpsimd.tensor_copy(out=g_col[:], in_=g_b[:])
+        x_factor = keep.tile([P, ROW_TILES, GROUPS], F32, name="x_factor")
+        by_quadrant = x_scale_all[:].rearrange("p (i k quadrant) -> p i k quadrant", i=ROW_TILES, k=GROUPS)
+        for quadrant in range(4):
+            lanes = slice(32 * quadrant, 32 * quadrant + 32)
+            nc.gpsimd.tensor_copy(out=x_factor[lanes], in_=by_quadrant[lanes, :, :, quadrant])
+        c_col = keep.tile([P, GROUPS, PACK], F32, name="c_col")
+        g_col = keep.tile([P, GROUPS, PACK], F32, name="g_col")
+        nc.gpsimd.tensor_copy(out=c_col[:], in_=c_words[:])
+        nc.gpsimd.tensor_copy(out=g_col[:], in_=g_words[:])
+        nc.gpsimd.tensor_scalar(half_pi[:], silu_zero[:], math.pi / 2, None, ALU.add)
 
-        x_il, x_codes, x_planes = {}, {}, {}
-        for h in range(2):
-            xi = keep.tile([P, 2, HALF, 4], BF16, name=f"x_il{h}", align_bytes=64)
-            x_il[h] = xi
-            for k in range(2):
-                xc = keep.tile([P, HALF], U32, name=f"x_codes{h}{k}", align_bytes=64)
-                xp = keep.tile([P, HALF], U8, name=f"x_planes{h}{k}", align_bytes=64)
-                x_codes[h, k], x_planes[h, k] = xc, xp
-        x_bf, x_t = {}, {}
-
-        def widen_x(i, on_scalar):
-            wide = work.tile([P, F], BF16, name="x_bf", bufs=6, align_bytes=64)
-            x_bf[i] = wide
-            if on_scalar:
-                nc.scalar.copy(out=wide[:], in_=x_raw[i][:].bitcast(E4M3))
-            else:
-                nc.vector.tensor_copy(out=wide[:], in_=x_raw[i][:].bitcast(E4M3))
-
-        def turn_x(i):
-            words = x_bf[i][:].bitcast(F32)
-            xt = psum.tile([P, 2, 2, P], F32, name="tp", bufs=3)
-            x_t[i] = xt
-            for k in range(2):
-                for u in range(2):
-                    nc.tensor.transpose(xt[:, k, u, :], words[:, 256 * k + u : 256 * (k + 1) : 2], ident[:])
-
-        def empty_x(i, on_scalar=False):
-            h, b = divmod(i, 4)
-            for k in range(2):
-                dst = x_il[h][:, k, P * b : P * (b + 1), :].rearrange("p n (u e) -> p n u e", e=2)
-                src = x_t[i][:, k].bitcast(BF16).rearrange("p u (n e) -> p n u e", e=2)
-                if on_scalar:
-                    nc.scalar.activation(out=dst, in_=src, func=ACT.Copy, scale=xsc[:, i, k : k + 1])
-                else:
-                    nc.vector.tensor_scalar(
-                        out=dst, in0=src, scalar1=xsc[:, i, k : k + 1], scalar2=None, op0=ALU.mult
-                    )
-
-        def quant_x(h, k):
-            nc.vector.quantize_mx(
-                out=x_codes[h, k][:].bitcast(E4M3X4),
-                scales=x_planes[h, k][:],
-                in_=x_il[h][:, k].rearrange("p n t -> p (n t)"),
-            )
-
-        w_perm = {}
-        wsc = []
-        for q in range(2):
-            wsc_q = keep.tile([P, 2, 4, P], U8, name=f"wsc{q}", align_bytes=64)
-            wsc.append(wsc_q)
-
-        def permute_w(q):
-            for k in range(2):
-                wp = keep.tile([P, 4, 256], U8, name=f"w_perm{k}{q}", align_bytes=64)
-                w_perm[k, q] = wp
-                nc.vector.tensor_copy(
-                    out=wp[:].rearrange("p t (m b) -> p t m b", b=2),
-                    in_=w_raw[q][:, k, :].rearrange("p (m t b) -> p t m b", t=4, b=2),
-                )
-
-        def permute_wsc(q):
-            nc.vector.tensor_copy(
-                out=wsc[q][:],
-                in_=wsc_raw[:, :, HALF * q : HALF * (q + 1)].rearrange("p k (m t) -> p k t m", t=4),
-            )
-
-        th, z_gained, z_il, z_codes, z_planes = {}, {}, {}, {}, {}
-        h_ps = {}
-
-        def multiply_w(h, q, t):
-            ps = psum.tile([P, HALF], F32, name="mm", bufs=5)
-            h_ps[h, q, t] = ps
-            for k in range(2):
-                nc.tensor.matmul_mx(
-                    out=ps[:],
-                    lhsT=w_perm[k, q][:, t, :].bitcast(E2M1X4),
-                    lhsT_scale=wsc[q][:, k, t, :],
-                    rhs=x_codes[h, k][:].bitcast(E4M3X4),
-                    rhs_scale=x_planes[h, k][:],
-                    start=(k == 0),
-                    stop=(k == 1),
-                )
-
-        def tanh_h(h, q, t):
-            if t == 0:
-                th_hq = work.tile([P, 4, HALF], F32, name="th", bufs=3, align_bytes=64)
-                th[h, q] = th_hq
-            nc.scalar.activation(
-                out=th[h, q][:, t, :], in_=h_ps[h, q, t][:], func=ACT.Tanh, bias=c_col[:, q, t : t + 1]
-            )
-
-        def gain_z(h, q, t, on_scalar):
-            if t == 0:
-                zg = work.tile([P, 4, HALF], BF16, name="z_gained", bufs=3, align_bytes=64)
-                z_gained[h, q] = zg
-            dst, src, factor = z_gained[h, q][:, t, :], th[h, q][:, t, :], g_col[:, q, t : t + 1]
-            if on_scalar:
-                nc.scalar.activation(out=dst, in_=src, func=ACT.Copy, scale=factor)
-            else:
-                nc.vector.tensor_scalar(out=dst, in0=src, scalar1=factor, scalar2=None, op0=ALU.mult)
-
-        def weave_z(h, q):
-            zi = work.tile([P, HALF, 4], BF16, name="z_il", bufs=3, align_bytes=64)
-            z_il[h, q] = zi
-            nc.vector.tensor_copy(
-                out=zi[:].rearrange("p (m i) t -> p m t i", i=4),
-                in_=z_gained[h, q][:].rearrange("p t (m i) -> p m t i", i=4),
-            )
-
-        def quant_z(h, q):
-            zc = keep.tile([P, HALF], U32, name=f"z_codes{q}{h}", align_bytes=64)
-            zp = keep.tile([P, HALF], U8, name=f"z_planes{q}{h}", align_bytes=64)
-            z_codes[q, h], z_planes[q, h] = zc, zp
-            nc.vector.quantize_mx(
-                out=zc[:].bitcast(E4M3X4), scales=zp[:], in_=z_il[h, q][:].rearrange("p n t -> p (n t)")
-            )
-
-        def heat(n):
-            for i in range(n):
-                ps = psum.tile([P, P], F32, name="mm", bufs=5)
-                nc.tensor.matmul(ps[:], lhsT=ident[:], rhs=ident[:], start=True, stop=True)
-
-        def heat_on(h, q, n):
-            for t in range(n):
-                ps = psum.tile([P, HALF], F32, name="mm", bufs=5)
-                src = z_gained[h, q]
-                nc.tensor.matmul(ps[:], lhsT=src[:, t, 0:P], rhs=src[:, t, :], start=True, stop=True)
-
-        half_pi = keep.tile([P, 1], F32, name="half_pi")
-        s_f = keep.tile([P, P], F32, name="s_f")
-        s_col = keep.tile([P, 8], F32, name="s_col")
-        s_turn = keep.tile([P, 8], F32, name="s_turn")
-        s_mean = keep.tile([P, 8], F32, name="s_mean")
-        s_nmean = keep.tile([P, 8], F32, name="s_nmean")
-        s_sq = keep.tile([P, 8], F32, name="s_sq")
-        th_q = keep.tile([P, 8], F32, name="th_q")
-        num = keep.tile([P, 8], F32, name="num")
-        den = keep.tile([P, 8], F32, name="den")
-        s_psi4 = keep.tile([P, 8], F32, name="s_psi4")
+        s_square = keep.tile([P, P], F32, name="s_square")
+        s_col = keep.tile([P, SLICE_TILES], F32, name="s_col")
+        s_turn = keep.tile([P, SLICE_TILES], F32, name="s_turn")
+        s_mean = keep.tile([P, SLICE_TILES], F32, name="s_mean")
+        s_minus = keep.tile([P, SLICE_TILES], F32, name="s_minus")
+        s_psi = keep.tile([P, SLICE_TILES], F32, name="s_psi")
+        s_two = keep.tile([P, SLICE_TILES], F32, name="s_two")
+        tanh_q = keep.tile([P, SLICE_TILES], F32, name="tanh_q")
+        num = keep.tile([P, SLICE_TILES], F32, name="num")
+        den = keep.tile([P, SLICE_TILES], F32, name="den")
 
         def prepare_s():
-            nc.gpsimd.tensor_scalar(half_pi[:], warm[:], math.pi / 2, None, ALU.add)
-            nc.gpsimd.tensor_copy(out=s_f[:], in_=s_rows[:])
-            s_ps = psum.tile([P, P], F32, name="tp", bufs=3)
-            nc.tensor.transpose(s_ps[:], s_f[:], ident[:])
-            nc.vector.tensor_copy(out=s_col[:], in_=s_ps[:, 0:8])
-            nc.gpsimd.tensor_tensor(s_sq[:], s_col[:], s_col[:], ALU.mult)
+            nc.gpsimd.tensor_copy(out=s_square[:], in_=s_rows[:])
+            s_bank = psum.tile([P, P], F32, name="turned", bufs=3)
+            nc.tensor.transpose(s_bank[:], s_square[:], ident[:])
+            nc.vector.tensor_copy(out=s_col[:], in_=s_bank[:, 0:SLICE_TILES])
+            nc.gpsimd.tensor_tensor(s_two[:], s_col[:], s_col[:], ALU.mult)
             nc.gpsimd.tensor_scalar(s_turn[:], s_col[:], 1.0 / TWO_PI, None, ALU.mult)
-            nc.gpsimd.tensor_scalar(s_mean[:], s_col[:], 4.0 / N, None, ALU.mult)
-            nc.gpsimd.tensor_scalar(s_nmean[:], s_col[:], -4.0 / N, None, ALU.mult)
-
-        def start_psi():
-            nc.scalar.activation(out=th_q[:], in_=s_sq[:], func=ACT.Tanh, scale=0.25)
+            nc.gpsimd.tensor_scalar(s_mean[:], s_col[:], 4.0 / ROWS, None, ALU.mult)
+            nc.gpsimd.tensor_scalar(s_minus[:], s_col[:], -4.0 / ROWS, None, ALU.mult)
 
         def prepare_psi():
-            nc.vector.tensor_scalar(den[:], th_q[:], 1.0, None, ALU.add)
-            nc.vector.tensor_scalar(num[:], th_q[:], -1.0, 1.0, ALU.mult, ALU.add)
+            nc.scalar.activation(out=tanh_q[:], in_=s_two[:], func=ACT.Tanh, scale=0.25)
+            nc.gpsimd.tensor_scalar(den[:], tanh_q[:], 1.0, None, ALU.add)
+            nc.gpsimd.tensor_scalar(num[:], tanh_q[:], -1.0, 1.0, ALU.mult, ALU.add)
+
+        def finish_psi():
             nc.vector.reciprocal(den[:], den[:])
             nc.gpsimd.tensor_tensor(num[:], num[:], s_col[:], ALU.mult)
             nc.gpsimd.tensor_tensor(num[:], num[:], den[:], ALU.mult)
-            nc.gpsimd.tensor_scalar(s_psi4[:], num[:], 4.0, None, ALU.mult)
+            nc.gpsimd.tensor_scalar(s_psi[:], num[:], 4.0, None, ALU.mult)
 
-        out_view = out.rearrange("(b p) m -> p b m", p=P)
-        u_ps, turn_t, r_t, sin_t, cos_t, sin_sum, cos_sum = {}, {}, {}, {}, {}, {}, {}
-        abs_t, sin_s, cos_s, o_ps, o_sb = {}, {}, {}, {}, {}
+        x_grouped, x_codes, x_planes = {}, {}, {}
+        for h in range(HALVES):
+            grouped = keep.tile([P, GROUPS, HALF, PACK], BF16, name=f"x_grouped{h}", align_bytes=64)
+            x_grouped[h] = grouped
+            for k in range(GROUPS):
+                codes = keep.tile([P, HALF], U32, name=f"x_codes{h}{k}", align_bytes=64)
+                plane = keep.tile([P, HALF], U8, name=f"x_plane{h}{k}", align_bytes=64)
+                x_codes[h, k], x_planes[h, k] = codes, plane
+        x_wide, x_turned = {}, {}
+
+        def widen_x(i):
+            wide = work.tile([P, FEATURES], BF16, name="x_wide", bufs=6, align_bytes=64)
+            x_wide[i] = wide
+            nc.scalar.copy(out=wide[:], in_=x_raw[i][:].bitcast(E4M3))
+
+        def turn_x(i):
+            words = x_wide[i][:].bitcast(F32)
+            bank = psum.tile([P, GROUPS, 2, P], F32, name="turned", bufs=3)
+            x_turned[i] = bank
+            for k in range(GROUPS):
+                for u in range(2):
+                    first = GROUP // 2 * k + u
+                    nc.tensor.transpose(bank[:, k, u, :], words[:, first : GROUP // 2 * (k + 1) : 2], ident[:])
+
+        def scale_x(i):
+            h, tile = divmod(i, HALF_TILES)
+            for k in range(GROUPS):
+                rows = x_grouped[h][:, k, P * tile : P * (tile + 1), :]
+                nc.vector.tensor_scalar(
+                    out=rows.rearrange("p n (u e) -> p n u e", e=2),
+                    in0=x_turned[i][:, k].bitcast(BF16).rearrange("p u (n e) -> p n u e", e=2),
+                    scalar1=x_factor[:, i, k : k + 1],
+                    scalar2=None,
+                    op0=ALU.mult,
+                )
+
+        def quantise_x(h):
+            for k in range(GROUPS):
+                nc.vector.quantize_mx(
+                    out=x_codes[h, k][:].bitcast(E4M3X4),
+                    scales=x_planes[h, k][:],
+                    in_=x_grouped[h][:, k].rearrange("p n t -> p (n t)"),
+                )
+
+        w_codes, w_planes = {}, {}
+
+        def permute_w_codes(q):
+            codes = keep.tile([P, PACK, GROUPS, 2 * P], U8, name=f"w_codes{q}", align_bytes=64)
+            w_codes[q] = codes
+            nc.vector.tensor_copy(
+                out=codes[:].rearrange("p t k (m b) -> p t (k m) b", b=2),
+                in_=w_raw[q][:].rearrange("p k n -> p (k n)").rearrange("p (m t b) -> p t m b", t=PACK, b=2),
+            )
+
+        def permute_w_scales(q):
+            plane = keep.tile([P, GROUPS, PACK, P], U8, name=f"w_plane{q}", align_bytes=64)
+            w_planes[q] = plane
+            nc.vector.tensor_copy(
+                out=plane[:],
+                in_=w_scale_rows[:, :, GROUP * q : GROUP * (q + 1)].rearrange("p k (m t) -> p k t m", t=PACK),
+            )
+
+        embedded, z_grouped, z_codes, z_planes = {}, {}, {}, {}
+
+        def embed(h, q):
+            tanh_h = work.tile([P, PACK, HALF], F32, name="tanh_h", bufs=3, align_bytes=64)
+            embedded[h, q] = tanh_h
+            for t in range(PACK):
+                bank = psum.tile([P, HALF], F32, name="product", bufs=5)
+                for k in range(GROUPS):
+                    nc.tensor.matmul_mx(
+                        out=bank[:],
+                        lhsT=w_codes[q][:, t, k, :].bitcast(E2M1X4),
+                        lhsT_scale=w_planes[q][:, k, t, :],
+                        rhs=x_codes[h, k][:].bitcast(E4M3X4),
+                        rhs_scale=x_planes[h, k][:],
+                        start=(k == 0),
+                        stop=(k == GROUPS - 1),
+                    )
+                nc.scalar.activation(
+                    out=tanh_h[:, t, :], in_=bank[:], func=ACT.Tanh, bias=c_col[:, q, t : t + 1]
+                )
+
+        def gain_z(h, q):
+            grouped = work.tile([P, HALF, PACK], BF16, name="z_grouped", bufs=3, align_bytes=64)
+            z_grouped[h, q] = grouped
+            nc.vector.tensor_tensor(
+                out=grouped[:].rearrange("p (m i) t -> p m t i", i=4),
+                in0=embedded[h, q][:].rearrange("p t (m i) -> p m t i", i=4),
+                in1=g_col[:, q, :].unsqueeze(1).unsqueeze(3).to_broadcast([P, HALF // 4, PACK, 4]),
+                op=ALU.mult,
+            )
+
+        def quantise_z(h, q):
+            codes = keep.tile([P, HALF], U32, name=f"z_codes{q}{h}", align_bytes=64)
+            plane = keep.tile([P, HALF], U8, name=f"z_plane{q}{h}", align_bytes=64)
+            z_codes[q, h], z_planes[q, h] = codes, plane
+            nc.vector.quantize_mx(
+                out=codes[:].bitcast(E4M3X4),
+                scales=plane[:],
+                in_=z_grouped[h, q][:].rearrange("p n t -> p (n t)"),
+            )
+
+        products, turns, rests, sizes, sines, cosines = {}, {}, {}, {}, {}, {}
+        sine_sums, cosine_sums, cosine_factor, sine_factor = {}, {}, {}, {}
+        cosine_terms, sine_terms, banks, results = {}, {}, {}, {}
 
         def multiply_a(j, h):
-            ps = psum.tile([P, HALF], F32, name="mm", bufs=5)
-            u_ps[j, h] = ps
-            for q in range(2):
+            bank = psum.tile([P, HALF], F32, name="product", bufs=5)
+            products[j, h] = bank
+            for q in range(GROUPS):
                 nc.tensor.matmul_mx(
-                    out=ps[:],
-                    lhsT=a_raw[:, q, 256 * j : 256 * (j + 1)].bitcast(E2M1X4),
-                    lhsT_scale=asc[:, q, P * j : P * (j + 1)],
+                    out=bank[:],
+                    lhsT=a_codes[:, q, 2 * P * j : 2 * P * (j + 1)].bitcast(E2M1X4),
+                    lhsT_scale=a_scale_tile[:, q, P * j : P * (j + 1)],
                     rhs=z_codes[q, h][:].bitcast(E4M3X4),
                     rhs_scale=z_planes[q, h][:],
                     start=(q == 0),
-                    stop=(q == 1),
+                    stop=(q == GROUPS - 1),
                 )
 
         def count_turns(j, h):
-            tt = work.tile([P, HALF], I32, name="turns", bufs=5)
-            turn_t[j, h] = tt
-            nc.vector.tensor_scalar(tt[:], u_ps[j, h][:], s_turn[:, j : j + 1], None, ALU.mult)
+            whole = work.tile([P, HALF], I32, name="whole", bufs=5)
+            turns[j, h] = whole
+            nc.vector.tensor_scalar(whole[:], products[j, h][:], s_turn[:, j : j + 1], None, ALU.mult)
 
         def take_turns(j, h):
-            if h == 0:
-                rr = work.tile([P, N], F32, name="r", bufs=5)
-                r_t[j] = rr
+            if j not in rests:
+                rest = work.tile([P, ROWS], F32, name="rest", bufs=5)
+                rests[j] = rest
             nc.vector.scalar_tensor_tensor(
-                out=r_t[j][:, HALF * h : HALF * (h + 1)],
-                in0=u_ps[j, h][:],
+                out=rests[j][:, HALF * h : HALF * (h + 1)],
+                in0=products[j, h][:],
                 scalar=s_turn[:, j : j + 1],
-                in1=turn_t[j, h][:],
+                in1=turns[j, h][:],
                 op0=ALU.mult,
                 op1=ALU.subtract,
             )
 
-        def sine(j, lo, hi):
-            ss = work.tile([P, 1], F32, name="sin_sum", bufs=8)
-            sin_sum[j].append(ss)
+        def find_sizes(j, lo, hi):
+            if lo == 0:
+                size = work.tile([P, ROWS], F32, name="size", bufs=2)
+                sine = work.tile([P, ROWS], F32, name="sine", bufs=5)
+                cosine = work.tile([P, ROWS], F32, name="cosine", bufs=5)
+                sizes[j], sines[j], cosines[j], sine_sums[j], cosine_sums[j] = size, sine, cosine, [], []
+            nc.scalar.activation(out=sizes[j][:, lo:hi], in_=rests[j][:, lo:hi], func=ACT.Abs)
+
+        def find_sines(j, lo, hi):
+            total = work.tile([P, 1], F32, name="sine_sum", bufs=8)
+            sine_sums[j].append(total)
             nc.scalar.activation(
-                out=sin_t[j][:, lo:hi], in_=r_t[j][:, lo:hi], func=ACT.Sin, scale=TWO_PI, accum_out=ss[:]
+                out=sines[j][:, lo:hi], in_=rests[j][:, lo:hi], func=ACT.Sin, scale=TWO_PI, accum_out=total[:]
             )
 
-        def cosine(j, lo, hi):
-            cs = work.tile([P, 1], F32, name="cos_sum", bufs=8)
-            cos_sum[j].append(cs)
+        def find_cosines(j, lo, hi):
+            total = work.tile([P, 1], F32, name="cosine_sum", bufs=8)
+            cosine_sums[j].append(total)
             nc.scalar.activation(
-                out=cos_t[j][:, lo:hi],
-                in_=abs_t[j][:, lo:hi],
+                out=cosines[j][:, lo:hi],
+                in_=sizes[j][:, lo:hi],
                 func=ACT.Sin,
                 scale=-TWO_PI,
                 bias=half_pi[:],
-                accum_out=cs[:],
+                accum_out=total[:],
             )
 
-        def magnitude(j, lo, hi):
-            if lo == 0:
-                ra = work.tile([P, N], F32, name="r_abs", bufs=2)
-                su = work.tile([P, N], F32, name="sin_u", bufs=5)
-                cu = work.tile([P, N], F32, name="cos_u", bufs=5)
-                abs_t[j], sin_t[j], cos_t[j], sin_sum[j], cos_sum[j] = ra, su, cu, [], []
-            nc.scalar.activation(out=abs_t[j][:, lo:hi], in_=r_t[j][:, lo:hi], func=ACT.Abs)
-
-        def trig(j, parts):
-            for lo, hi in parts:
-                magnitude(j, lo, hi)
-                sine(j, lo, hi)
-                cosine(j, lo, hi)
-
-        cos_k, sin_k = {}, {}
-
-        def cos_weight(j):
-            ck = sin_sum[j][0]
-            if len(sin_sum[j]) == 2:
+        def find_cosine_factor(j):
+            total = sine_sums[j][0]
+            if len(sine_sums[j]) == 2:
                 both = work.tile([P, 1], F32, name="both", bufs=4)
-                nc.scalar.activation(out=both[:], in_=ck[:], func=ACT.Identity, bias=sin_sum[j][1][:])
-                ck = both
-            cos_k[j] = ck[:]
+                nc.scalar.activation(out=both[:], in_=total[:], func=ACT.Identity, bias=sine_sums[j][1][:])
+                total = both
+            cosine_factor[j] = total[:]
 
-        def sin_weight(j):
-            sk = s_psi4[:, j : j + 1]
-            for n, cs in enumerate(cos_sum[j]):
-                nxt = work.tile([P, 1], F32, name="sin_k", bufs=6)
+        def find_sine_factor(j):
+            factor = s_psi[:, j : j + 1]
+            for total in cosine_sums[j]:
+                step = work.tile([P, 1], F32, name="sine_factor", bufs=6)
                 nc.scalar.activation(
-                    out=nxt[:], in_=cs[:], func=ACT.Identity, scale=s_nmean[:, j : j + 1], bias=sk
+                    out=step[:], in_=total[:], func=ACT.Identity, scale=s_minus[:, j : j + 1], bias=factor
                 )
-                sk = nxt[:]
-            sin_k[j] = sk
+                factor = step[:]
+            sine_factor[j] = factor
 
-        def weights(j):
-            cos_weight(j)
-            sin_weight(j)
-
-        diag_t = {}
-
-        def weigh(j, cos_on):
-            ck, sk = cos_k[j], sin_k[j]
-            if cos_on == "pe":
-                dg = work.tile([P, P], F32, name="diag", bufs=2)
-                diag_t[j] = dg
-                nc.gpsimd.tensor_scalar(dg[:], ident[:], ck, s_mean[:, j : j + 1], ALU.mult, ALU.mult)
-            else:
-                co = work.tile([P, N], F32, name="cos_s", bufs=2)
-                cos_s[j] = co
-                if cos_on == "v":
-                    nc.vector.tensor_scalar(co[:], cos_t[j][:], ck, s_mean[:, j : j + 1], ALU.mult, ALU.mult)
-                else:
-                    nc.gpsimd.tensor_scalar(co[:], cos_t[j][:], ck, s_mean[:, j : j + 1], ALU.mult, ALU.mult)
-            si = work.tile([P, N], F32, name="sin_s", bufs=2)
-            sin_s[j] = si
-            nc.gpsimd.tensor_scalar(si[:], sin_t[j][:], sk, 0.0, ALU.mult, ALU.add)
-
-        def weigh_on_vector(j, lo, hi):
-            nc.vector.tensor_scalar(
-                cos_s[j][:, lo:hi], cos_t[j][:, lo:hi], cos_k[j], s_mean[:, j : j + 1], ALU.mult, ALU.mult
+        def weigh(engine, j, lo, hi):
+            if lo == 0:
+                cosine_term = work.tile([P, ROWS], F32, name="cosine_term", bufs=2)
+                sine_term = work.tile([P, ROWS], F32, name="sine_term", bufs=2)
+                cosine_terms[j], sine_terms[j] = cosine_term, sine_term
+            engine.tensor_scalar(
+                cosine_terms[j][:, lo:hi],
+                cosines[j][:, lo:hi],
+                cosine_factor[j],
+                s_mean[:, j : j + 1],
+                ALU.mult,
+                ALU.mult,
             )
-            nc.vector.tensor_scalar(sin_s[j][:, lo:hi], sin_t[j][:, lo:hi], sin_k[j], None, ALU.mult)
+            engine.tensor_scalar(
+                sine_terms[j][:, lo:hi], sines[j][:, lo:hi], sine_factor[j], 0.0, ALU.mult, ALU.add
+            )
 
-        def weighed_tiles(j):
-            co = work.tile([P, N], F32, name="cos_s", bufs=2)
-            si = work.tile([P, N], F32, name="sin_s", bufs=2)
-            cos_s[j], sin_s[j] = co, si
-
-        def turn_out(j, hb):
-            ps = psum.tile([P, 4, P], F32, name="tp", bufs=3)
-            o_ps[j, hb] = ps
-            for b in range(4):
-                blk = slice(P * (4 * hb + b), P * (4 * hb + b + 1))
-                if j in diag_t:
-                    nc.tensor.matmul(ps[:, b, :], lhsT=cos_t[j][:, blk], rhs=diag_t[j][:], start=True, stop=False)
-                else:
-                    nc.tensor.matmul(
-                        ps[:, b, :], lhsT=cos_s[j][:, blk], rhs=ident[:], is_transpose=True, start=True, stop=False
-                    )
+        def turn_out(j, h):
+            bank = psum.tile([P, HALF_TILES, P], F32, name="turned", bufs=3)
+            banks[j, h] = bank
+            for tile in range(HALF_TILES):
+                rows = slice(HALF * h + P * tile, HALF * h + P * (tile + 1))
                 nc.tensor.matmul(
-                    ps[:, b, :], lhsT=sin_s[j][:, blk], rhs=ident[:], is_transpose=True, start=False, stop=True
+                    bank[:, tile, :],
+                    lhsT=cosine_terms[j][:, rows],
+                    rhs=ident[:],
+                    is_transpose=True,
+                    start=True,
+                    stop=False,
+                )
+                nc.tensor.matmul(
+                    bank[:, tile, :],
+                    lhsT=sine_terms[j][:, rows],
+                    rhs=ident[:],
+                    is_transpose=True,
+                    start=False,
+                    stop=True,
                 )
 
-        def leave(j, hb, on_scalar=False):
-            if hb == 0:
-                ob = work.tile([P, 8, P], F32, name="o_sb", bufs=3)
-                o_sb[j] = ob
-            dst = o_sb[j][:, 4 * hb : 4 * hb + 4, :]
-            if on_scalar:
-                nc.scalar.copy(out=dst, in_=o_ps[j, hb][:])
-            else:
-                nc.vector.tensor_copy(out=dst, in_=o_ps[j, hb][:])
-            nc.sync.dma_start(
-                out=out_view[:, 4 * hb : 4 * hb + 4, P * j : P * (j + 1)], in_=dst
-            )
+        out_tiles = out.rearrange("(tile p) m -> p tile m", p=P)
 
-        E = 2
-        LAG_T, LAG_L = 3, 4
-        COS = ["g","g","g","g","g","g","g","v"]
-        LEAVE_S = ()
-        SEQ = [0, 2, 1, 3, 4, 5, 6, 7]
-        WIDE_V = [2, 3]
-        GAIN_S = {(0, 0): (), (0, 1): (), (1, 0): (), (1, 1): (1, 2, 3)}
-        EMPTY_S = [0, 1]
+        def leave(copy, j, h):
+            if h == 0:
+                result = work.tile([P, ROW_TILES, P], F32, name="result", bufs=4)
+                results[j] = result
+            tiles = slice(HALF_TILES * h, HALF_TILES * (h + 1))
+            copy(out=results[j][:, tiles, :], in_=banks[j, h][:])
+            nc.sync.dma_start(out=out_tiles[:, tiles, P * j : P * (j + 1)], in_=results[j][:, tiles, :])
 
-        def s1(h, q):
-            for t in range(4):
-                multiply_w(h, q, t)
-                tanh_h(h, q, t)
-
-        def widen(i):
-            widen_x(i, i not in WIDE_V)
-
-        def empty(i):
-            empty_x(i, i in EMPTY_S)
-
-        def gain(h, q):
-            for t in range(4):
-                gain_z(h, q, t, t in GAIN_S[h, q])
-
-        heat(6)
-        permute_w(0)
-        widen(0)
-        widen(1)
-        turn_x(0)
-        heat(1)
-        empty(0)
-        widen(2)
-        turn_x(1)
-        heat(1)
-        permute_wsc(0)
-        empty(1)
-        widen(3)
-        turn_x(2)
-        heat(1)
-        turn_x(3)
-        heat(1)
-        empty(2)
-        empty(3)
-        for k in range(2):
-            quant_x(0, k)
+        permute_w_codes(0)
+        for i in range(HALF_TILES):
+            widen_x(i)
+            turn_x(i)
+            scale_x(i)
+            if i == 0:
+                permute_w_scales(0)
+        quantise_x(0)
         prepare_s()
-        widen(4)
-        widen(5)
-        permute_w(1)
-        permute_wsc(1)
-        s1(0, 0)
-        turn_x(4)
-        turn_x(5)
-        empty(4)
-        empty(5)
-        widen(6)
-        widen(7)
-        s1(0, 1)
-        start_psi()
-        turn_x(6)
-        turn_x(7)
-        gain(0, 0)
-        empty(6)
-        empty(7)
-        for k in range(2):
-            quant_x(1, k)
-        weave_z(0, 0)
-        s1(1, 0)
-        gain(0, 1)
+        for i in (4, 5):
+            widen_x(i)
+            turn_x(i)
+        permute_w_codes(1)
+        permute_w_scales(1)
+        embed(0, 0)
+        for i in (4, 5):
+            scale_x(i)
+        for i in (6, 7):
+            widen_x(i)
+        embed(0, 1)
         prepare_psi()
-        quant_z(0, 0)
-        weave_z(0, 1)
-        s1(1, 1)
-        gain(1, 0)
-        quant_z(0, 1)
-        weave_z(1, 0)
-        heat_on(1, 0, 2)
-        for j in range(E):
+        for i in (6, 7):
+            turn_x(i)
+        gain_z(0, 0)
+        for i in (6, 7):
+            scale_x(i)
+        quantise_x(1)
+        embed(1, 0)
+        gain_z(0, 1)
+        finish_psi()
+        quantise_z(0, 0)
+        embed(1, 1)
+        quantise_z(0, 1)
+        for j in range(EARLY):
             multiply_a(j, 0)
-        gain(1, 1)
-        for j in range(E):
+        gain_z(1, 0)
+        for j in range(EARLY):
             count_turns(j, 0)
-        quant_z(1, 0)
-        for j in range(E):
+        for j in range(EARLY):
             take_turns(j, 0)
-            trig(j, [(0, HALF)])
-        weave_z(1, 1)
-        quant_z(1, 1)
+            find_sizes(j, 0, HALF)
+            find_sines(j, 0, HALF)
+            find_cosines(j, 0, HALF)
+        gain_z(1, 1)
+        quantise_z(1, 0)
+        quantise_z(1, 1)
 
-        def parts(j):
-            return [1] if j < E else [0, 1]
+        def halves_left(j):
+            return [1] if j < EARLY else [0, 1]
 
-        coming = [(j, h) for j in SEQ for h in parts(j)]
+        coming = [(j, h) for j in range(SLICE_TILES) for h in halves_left(j)]
         for n in range(2):
             multiply_a(*coming.pop(0))
-        for i in range(8):
-            j = SEQ[i]
-            w = SEQ[i - LAG_T] if i >= LAG_T else None
-            v = SEQ[i - LAG_L] if i >= LAG_L else None
-            for h in parts(j):
+        for j in range(SLICE_TILES):
+            last = j == SLICE_TILES - 1
+            for h in halves_left(j):
                 count_turns(j, h)
-            if len(parts(j)) == 1 and v is not None:
-                leave(v, 0, (v, 0) in LEAVE_S)
-            for h in parts(j):
+            for h in halves_left(j):
                 take_turns(j, h)
-            if i < 7:
-                trig(j, [(HALF, N)] if j < E else [(0, N)])
-                weights(j)
-                if i < 6:
-                    weigh(j, COS[j])
-            if len(parts(j)) == 2 and v is not None:
-                leave(v, 0, (v, 0) in LEAVE_S)
-            if v is not None:
-                leave(v, 1, (v, 1) in LEAVE_S)
-            for hb in range(2):
-                if len(coming) > 0 and i >= 0:
+            lo = HALF if j < EARLY else 0
+            find_sizes(j, lo, ROWS)
+            find_sines(j, lo, ROWS)
+            if last:
+                find_cosine_factor(j)
+                for h in range(HALVES):
+                    find_cosines(j, HALF * h, HALF * (h + 1))
+            else:
+                find_cosines(j, lo, ROWS)
+                find_cosine_factor(j)
+            find_sine_factor(j)
+            if j < SLICE_TILES - VECTOR_TILES:
+                weigh(nc.gpsimd, j, 0, ROWS)
+            for h in range(HALVES):
+                if j >= LEAVE_LAG:
+                    leave(nc.vector.tensor_copy, j - LEAVE_LAG, h)
+            for h in range(HALVES):
+                if coming:
                     multiply_a(*coming.pop(0))
-                if w is not None:
-                    heat(2)
-                    turn_out(w, hb)
-        j, w = SEQ[7], SEQ[6]
-        magnitude(j, 0, N)
-        sine(j, 0, N)
-        cos_weight(j)
-        for lo in (0, HALF):
-            cosine(j, lo, lo + HALF)
-        sin_weight(j)
-        for v in range(8 - LAG_T, 6):
-            for hb in range(2):
-                heat(2)
-                turn_out(SEQ[v], hb)
-        weighed_tiles(w)
-        weigh_on_vector(w, 0, N)
-        for hb in range(2):
-            heat(2)
-            turn_out(w, hb)
-        for v in range(8 - LAG_L, 6):
-            for hb in range(2):
-                leave(SEQ[v], hb, (SEQ[v], hb) in LEAVE_S)
-        weighed_tiles(j)
-        leave(w, 0, False)
-        for hb in range(2):
-            heat(2)
-            weigh_on_vector(j, HALF * hb, HALF * (hb + 1))
-            turn_out(j, hb)
-        leave(w, 1, True)
-        leave(j, 0, True)
-        leave(j, 1, False)
+                if j >= TURN_LAG:
+                    turn_out(j - TURN_LAG, h)
+
+        before, last = SLICE_TILES - 2, SLICE_TILES - 1
+        for j in range(SLICE_TILES - TURN_LAG, before):
+            for h in range(HALVES):
+                turn_out(j, h)
+        weigh(nc.vector, before, 0, ROWS)
+        for h in range(HALVES):
+            turn_out(before, h)
+        for j in range(SLICE_TILES - LEAVE_LAG, before):
+            for h in range(HALVES):
+                leave(nc.vector.tensor_copy, j, h)
+        leave(nc.vector.tensor_copy, before, 0)
+        for h in range(HALVES):
+            weigh(nc.vector, last, HALF * h, HALF * (h + 1))
+            turn_out(last, h)
+        leave(nc.scalar.copy, before, 1)
+        leave(nc.scalar.copy, last, 0)
+        leave(nc.vector.tensor_copy, last, 1)

import math
from contextlib import ExitStack

import concourse.mybir as mybir
from concourse.masks import make_identity

ROWS, FEATURES, CHANNELS, SLICES = 1024, 1024, 1024, 1024
FLOPS = 2 * ROWS * FEATURES * CHANNELS + 2 * ROWS * CHANNELS * SLICES

F32 = mybir.dt.float32
BF16 = mybir.dt.bfloat16
I32 = mybir.dt.int32
U32 = mybir.dt.uint32
U8 = mybir.dt.uint8
E4M3 = mybir.dt.float8_e4m3fn
E4M3X4 = mybir.dt.float8_e4m3fn_x4
E2M1X4 = mybir.dt.float4_e2m1fn_x4
ALU = mybir.AluOpType
ACT = mybir.ActivationFunctionType

P = 128
PACK = 4
GROUP = P * PACK
GROUPS = 2
HALF = 512
HALVES = ROWS // HALF
ROW_TILES = ROWS // P
HALF_TILES = HALF // P
SLICE_TILES = SLICES // P
TWO_PI = 2.0 * math.pi

EARLY = 2
TURN_LAG = 3
LEAVE_LAG = 4
VECTOR_TILES = 2


def tile_lejepasigregrandomknotslicegrad_d2p_kernel(
    tc, x_bytes, x_scale, w_words, w_scales, c, g, a_words, a_scales, s, out
):
    nc = tc.nc
    with ExitStack() as ctx:
        keep = ctx.enter_context(tc.tile_pool(name="keep", bufs=1))
        work = ctx.enter_context(tc.tile_pool(name="work", bufs=2))
        psum = ctx.enter_context(tc.psum_pool(name="psum", bufs=1))
        ctx.enter_context(tc.manual_schedule())

        zero = keep.tile([P, 1], F32, name="zero")
        silu_zero = keep.tile([P, 1], F32, name="silu_zero")
        half_pi = keep.tile([P, 1], F32, name="half_pi")
        ident = keep.tile([P, P], F32, name="ident")
        nc.vector.memset(zero[:], 0.0)

        w_scale_rows = keep.tile([P, GROUPS, CHANNELS], U8, name="w_scale_rows", align_bytes=64)
        a_scale_tile = keep.tile([P, GROUPS, SLICES], U8, name="a_scale_tile", align_bytes=64)
        nc.vector.memset(w_scale_rows[:].bitcast(I32), 0)
        s_rows = keep.tile([P, P], BF16, name="s_rows")
        nc.gpsimd.memset(s_rows[:], 0.0)
        make_identity(nc, ident[:])
        nc.gpsimd.memset(a_scale_tile[:].bitcast(I32), 0)

        x_scale_all = keep.tile([P, ROW_TILES * 8], F32, name="x_scale_all")
        c_words = keep.tile([P, GROUPS, PACK], BF16, name="c_words")
        g_words = keep.tile([P, GROUPS, PACK], BF16, name="g_words")
        nc.scalar.dma_start(out=x_scale_all[:], in_=x_scale.rearrange("i j -> (i j)").partition_broadcast(P))
        nc.scalar.activation(out=silu_zero[:], in_=zero[:], func=ACT.Silu)
        nc.scalar.dma_start(out=s_rows[0:SLICE_TILES, :], in_=s.rearrange("(j p) -> j p", p=P))
        nc.scalar.dma_start(out=c_words[:], in_=c.rearrange("(q p t) -> p q t", p=P, t=PACK))
        nc.scalar.dma_start(out=g_words[:], in_=g.rearrange("(q p t) -> p q t", p=P, t=PACK))

        x_raw = []
        for i in range(ROW_TILES):
            x_raw_i = keep.tile([P, FEATURES], U8, name=f"x_raw{i}", align_bytes=64)
            x_raw.append(x_raw_i)
        w_raw = []
        for q in range(GROUPS):
            w_raw_q = keep.tile([P, GROUPS, 2 * GROUP], U8, name=f"w_raw{q}", align_bytes=64)
            w_raw.append(w_raw_q)
        a_codes = keep.tile([P, GROUPS, 2 * SLICES], U8, name="a_codes", align_bytes=64)

        def load_x(i):
            nc.sync.dma_start(out=x_raw[i][:], in_=x_bytes[P * i : P * (i + 1), :])

        def load_w(q):
            columns = w_words.rearrange("k p b -> p k b")[:, :, 2 * GROUP * q : 2 * GROUP * (q + 1)]
            nc.sync.dma_start(out=w_raw[q][:].bitcast(I32), in_=columns.bitcast(I32))

        def load_scale_rows(tile, rows):
            for quadrant in range(4):
                nc.sync.dma_start(
                    out=tile[32 * quadrant : 32 * quadrant + 4].bitcast(I32),
                    in_=rows[:, 4 * quadrant : 4 * quadrant + 4, :].rearrange("k r n -> r k n").bitcast(I32),
                )

        load_w(0)
        for i in range(3):
            load_x(i)
        load_scale_rows(w_scale_rows, w_scales)
        load_x(3)
        load_x(4)
        load_w(1)
        for i in range(5, ROW_TILES):
            load_x(i)
        nc.sync.dma_start(out=a_codes[:].bitcast(I32), in_=a_words.rearrange("k p b -> p k b").bitcast(I32))
        load_scale_rows(a_scale_tile, a_scales)

        x_factor = keep.tile([P, ROW_TILES, GROUPS], F32, name="x_factor")
        by_quadrant = x_scale_all[:].rearrange("p (i k quadrant) -> p i k quadrant", i=ROW_TILES, k=GROUPS)
        for quadrant in range(4):
            lanes = slice(32 * quadrant, 32 * quadrant + 32)
            nc.gpsimd.tensor_copy(out=x_factor[lanes], in_=by_quadrant[lanes, :, :, quadrant])
        c_col = keep.tile([P, GROUPS, PACK], F32, name="c_col")
        g_col = keep.tile([P, GROUPS, PACK], F32, name="g_col")
        nc.gpsimd.tensor_copy(out=c_col[:], in_=c_words[:])
        nc.gpsimd.tensor_copy(out=g_col[:], in_=g_words[:])
        nc.gpsimd.tensor_scalar(half_pi[:], silu_zero[:], math.pi / 2, None, ALU.add)

        s_square = keep.tile([P, P], F32, name="s_square")
        s_col = keep.tile([P, SLICE_TILES], F32, name="s_col")
        s_turn = keep.tile([P, SLICE_TILES], F32, name="s_turn")
        s_mean = keep.tile([P, SLICE_TILES], F32, name="s_mean")
        s_minus = keep.tile([P, SLICE_TILES], F32, name="s_minus")
        s_psi = keep.tile([P, SLICE_TILES], F32, name="s_psi")
        s_two = keep.tile([P, SLICE_TILES], F32, name="s_two")
        tanh_q = keep.tile([P, SLICE_TILES], F32, name="tanh_q")
        num = keep.tile([P, SLICE_TILES], F32, name="num")
        den = keep.tile([P, SLICE_TILES], F32, name="den")

        def prepare_s():
            nc.gpsimd.tensor_copy(out=s_square[:], in_=s_rows[:])
            s_bank = psum.tile([P, P], F32, name="turned", bufs=3)
            nc.tensor.transpose(s_bank[:], s_square[:], ident[:])
            nc.vector.tensor_copy(out=s_col[:], in_=s_bank[:, 0:SLICE_TILES])
            nc.gpsimd.tensor_tensor(s_two[:], s_col[:], s_col[:], ALU.mult)
            nc.gpsimd.tensor_scalar(s_turn[:], s_col[:], 1.0 / TWO_PI, None, ALU.mult)
            nc.gpsimd.tensor_scalar(s_mean[:], s_col[:], 4.0 / ROWS, None, ALU.mult)
            nc.gpsimd.tensor_scalar(s_minus[:], s_col[:], -4.0 / ROWS, None, ALU.mult)

        def prepare_psi():
            nc.scalar.activation(out=tanh_q[:], in_=s_two[:], func=ACT.Tanh, scale=0.25)
            nc.gpsimd.tensor_scalar(den[:], tanh_q[:], 1.0, None, ALU.add)
            nc.gpsimd.tensor_scalar(num[:], tanh_q[:], -1.0, 1.0, ALU.mult, ALU.add)

        def finish_psi():
            nc.vector.reciprocal(den[:], den[:])
            nc.gpsimd.tensor_tensor(num[:], num[:], s_col[:], ALU.mult)
            nc.gpsimd.tensor_tensor(num[:], num[:], den[:], ALU.mult)
            nc.gpsimd.tensor_scalar(s_psi[:], num[:], 4.0, None, ALU.mult)

        x_grouped, x_codes, x_planes = {}, {}, {}
        for h in range(HALVES):
            grouped = keep.tile([P, GROUPS, HALF, PACK], BF16, name=f"x_grouped{h}", align_bytes=64)
            x_grouped[h] = grouped
            for k in range(GROUPS):
                codes = keep.tile([P, HALF], U32, name=f"x_codes{h}{k}", align_bytes=64)
                plane = keep.tile([P, HALF], U8, name=f"x_plane{h}{k}", align_bytes=64)
                x_codes[h, k], x_planes[h, k] = codes, plane
        x_wide, x_turned = {}, {}

        def widen_x(i):
            wide = work.tile([P, FEATURES], BF16, name="x_wide", bufs=6, align_bytes=64)
            x_wide[i] = wide
            nc.scalar.copy(out=wide[:], in_=x_raw[i][:].bitcast(E4M3))

        def turn_x(i):
            words = x_wide[i][:].bitcast(F32)
            bank = psum.tile([P, GROUPS, 2, P], F32, name="turned", bufs=3)
            x_turned[i] = bank
            for k in range(GROUPS):
                for u in range(2):
                    first = GROUP // 2 * k + u
                    nc.tensor.transpose(bank[:, k, u, :], words[:, first : GROUP // 2 * (k + 1) : 2], ident[:])

        def scale_x(i):
            h, tile = divmod(i, HALF_TILES)
            for k in range(GROUPS):
                rows = x_grouped[h][:, k, P * tile : P * (tile + 1), :]
                nc.vector.tensor_scalar(
                    out=rows.rearrange("p n (u e) -> p n u e", e=2),
                    in0=x_turned[i][:, k].bitcast(BF16).rearrange("p u (n e) -> p n u e", e=2),
                    scalar1=x_factor[:, i, k : k + 1],
                    scalar2=None,
                    op0=ALU.mult,
                )

        def quantise_x(h):
            for k in range(GROUPS):
                nc.vector.quantize_mx(
                    out=x_codes[h, k][:].bitcast(E4M3X4),
                    scales=x_planes[h, k][:],
                    in_=x_grouped[h][:, k].rearrange("p n t -> p (n t)"),
                )

        w_codes, w_planes = {}, {}

        def permute_w_codes(q):
            codes = keep.tile([P, PACK, GROUPS, 2 * P], U8, name=f"w_codes{q}", align_bytes=64)
            w_codes[q] = codes
            nc.vector.tensor_copy(
                out=codes[:].rearrange("p t k (m b) -> p t (k m) b", b=2),
                in_=w_raw[q][:].rearrange("p k n -> p (k n)").rearrange("p (m t b) -> p t m b", t=PACK, b=2),
            )

        def permute_w_scales(q):
            plane = keep.tile([P, GROUPS, PACK, P], U8, name=f"w_plane{q}", align_bytes=64)
            w_planes[q] = plane
            nc.vector.tensor_copy(
                out=plane[:],
                in_=w_scale_rows[:, :, GROUP * q : GROUP * (q + 1)].rearrange("p k (m t) -> p k t m", t=PACK),
            )

        embedded, z_grouped, z_codes, z_planes = {}, {}, {}, {}

        def embed(h, q):
            tanh_h = work.tile([P, PACK, HALF], F32, name="tanh_h", bufs=3, align_bytes=64)
            embedded[h, q] = tanh_h
            for t in range(PACK):
                bank = psum.tile([P, HALF], F32, name="product", bufs=5)
                for k in range(GROUPS):
                    nc.tensor.matmul_mx(
                        out=bank[:],
                        lhsT=w_codes[q][:, t, k, :].bitcast(E2M1X4),
                        lhsT_scale=w_planes[q][:, k, t, :],
                        rhs=x_codes[h, k][:].bitcast(E4M3X4),
                        rhs_scale=x_planes[h, k][:],
                        start=(k == 0),
                        stop=(k == GROUPS - 1),
                    )
                nc.scalar.activation(
                    out=tanh_h[:, t, :], in_=bank[:], func=ACT.Tanh, bias=c_col[:, q, t : t + 1]
                )

        def gain_z(h, q):
            grouped = work.tile([P, HALF, PACK], BF16, name="z_grouped", bufs=3, align_bytes=64)
            z_grouped[h, q] = grouped
            nc.vector.tensor_tensor(
                out=grouped[:].rearrange("p (m i) t -> p m t i", i=4),
                in0=embedded[h, q][:].rearrange("p t (m i) -> p m t i", i=4),
                in1=g_col[:, q, :].unsqueeze(1).unsqueeze(3).to_broadcast([P, HALF // 4, PACK, 4]),
                op=ALU.mult,
            )

        def quantise_z(h, q):
            codes = keep.tile([P, HALF], U32, name=f"z_codes{q}{h}", align_bytes=64)
            plane = keep.tile([P, HALF], U8, name=f"z_plane{q}{h}", align_bytes=64)
            z_codes[q, h], z_planes[q, h] = codes, plane
            nc.vector.quantize_mx(
                out=codes[:].bitcast(E4M3X4),
                scales=plane[:],
                in_=z_grouped[h, q][:].rearrange("p n t -> p (n t)"),
            )

        products, turns, rests, sizes, sines, cosines = {}, {}, {}, {}, {}, {}
        sine_sums, cosine_sums, cosine_factor, sine_factor = {}, {}, {}, {}
        cosine_terms, sine_terms, banks, results = {}, {}, {}, {}

        def multiply_a(j, h):
            bank = psum.tile([P, HALF], F32, name="product", bufs=5)
            products[j, h] = bank
            for q in range(GROUPS):
                nc.tensor.matmul_mx(
                    out=bank[:],
                    lhsT=a_codes[:, q, 2 * P * j : 2 * P * (j + 1)].bitcast(E2M1X4),
                    lhsT_scale=a_scale_tile[:, q, P * j : P * (j + 1)],
                    rhs=z_codes[q, h][:].bitcast(E4M3X4),
                    rhs_scale=z_planes[q, h][:],
                    start=(q == 0),
                    stop=(q == GROUPS - 1),
                )

        def count_turns(j, h):
            whole = work.tile([P, HALF], I32, name="whole", bufs=5)
            turns[j, h] = whole
            nc.vector.tensor_scalar(whole[:], products[j, h][:], s_turn[:, j : j + 1], None, ALU.mult)

        def take_turns(j, h):
            if j not in rests:
                rest = work.tile([P, ROWS], F32, name="rest", bufs=5)
                rests[j] = rest
            nc.vector.scalar_tensor_tensor(
                out=rests[j][:, HALF * h : HALF * (h + 1)],
                in0=products[j, h][:],
                scalar=s_turn[:, j : j + 1],
                in1=turns[j, h][:],
                op0=ALU.mult,
                op1=ALU.subtract,
            )

        def find_sizes(j, lo, hi):
            if lo == 0:
                size = work.tile([P, ROWS], F32, name="size", bufs=2)
                sine = work.tile([P, ROWS], F32, name="sine", bufs=5)
                cosine = work.tile([P, ROWS], F32, name="cosine", bufs=5)
                sizes[j], sines[j], cosines[j], sine_sums[j], cosine_sums[j] = size, sine, cosine, [], []
            nc.scalar.activation(out=sizes[j][:, lo:hi], in_=rests[j][:, lo:hi], func=ACT.Abs)

        def find_sines(j, lo, hi):
            total = work.tile([P, 1], F32, name="sine_sum", bufs=8)
            sine_sums[j].append(total)
            nc.scalar.activation(
                out=sines[j][:, lo:hi], in_=rests[j][:, lo:hi], func=ACT.Sin, scale=TWO_PI, accum_out=total[:]
            )

        def find_cosines(j, lo, hi):
            total = work.tile([P, 1], F32, name="cosine_sum", bufs=8)
            cosine_sums[j].append(total)
            nc.scalar.activation(
                out=cosines[j][:, lo:hi],
                in_=sizes[j][:, lo:hi],
                func=ACT.Sin,
                scale=-TWO_PI,
                bias=half_pi[:],
                accum_out=total[:],
            )

        def find_cosine_factor(j):
            total = sine_sums[j][0]
            if len(sine_sums[j]) == 2:
                both = work.tile([P, 1], F32, name="both", bufs=4)
                nc.scalar.activation(out=both[:], in_=total[:], func=ACT.Identity, bias=sine_sums[j][1][:])
                total = both
            cosine_factor[j] = total[:]

        def find_sine_factor(j):
            factor = s_psi[:, j : j + 1]
            for total in cosine_sums[j]:
                step = work.tile([P, 1], F32, name="sine_factor", bufs=6)
                nc.scalar.activation(
                    out=step[:], in_=total[:], func=ACT.Identity, scale=s_minus[:, j : j + 1], bias=factor
                )
                factor = step[:]
            sine_factor[j] = factor

        def weigh(engine, j, lo, hi):
            if lo == 0:
                cosine_term = work.tile([P, ROWS], F32, name="cosine_term", bufs=2)
                sine_term = work.tile([P, ROWS], F32, name="sine_term", bufs=2)
                cosine_terms[j], sine_terms[j] = cosine_term, sine_term
            engine.tensor_scalar(
                cosine_terms[j][:, lo:hi],
                cosines[j][:, lo:hi],
                cosine_factor[j],
                s_mean[:, j : j + 1],
                ALU.mult,
                ALU.mult,
            )
            engine.tensor_scalar(
                sine_terms[j][:, lo:hi], sines[j][:, lo:hi], sine_factor[j], 0.0, ALU.mult, ALU.add
            )

        def turn_out(j, h):
            bank = psum.tile([P, HALF_TILES, P], F32, name="turned", bufs=3)
            banks[j, h] = bank
            for tile in range(HALF_TILES):
                rows = slice(HALF * h + P * tile, HALF * h + P * (tile + 1))
                nc.tensor.matmul(
                    bank[:, tile, :],
                    lhsT=cosine_terms[j][:, rows],
                    rhs=ident[:],
                    is_transpose=True,
                    start=True,
                    stop=False,
                )
                nc.tensor.matmul(
                    bank[:, tile, :],
                    lhsT=sine_terms[j][:, rows],
                    rhs=ident[:],
                    is_transpose=True,
                    start=False,
                    stop=True,
                )

        out_tiles = out.rearrange("(tile p) m -> p tile m", p=P)

        def leave(copy, j, h):
            if h == 0:
                result = work.tile([P, ROW_TILES, P], F32, name="result", bufs=4)
                results[j] = result
            tiles = slice(HALF_TILES * h, HALF_TILES * (h + 1))
            copy(out=results[j][:, tiles, :], in_=banks[j, h][:])
            nc.sync.dma_start(out=out_tiles[:, tiles, P * j : P * (j + 1)], in_=results[j][:, tiles, :])

        permute_w_codes(0)
        for i in range(HALF_TILES):
            widen_x(i)
            turn_x(i)
            scale_x(i)
            if i == 0:
                permute_w_scales(0)
        quantise_x(0)
        prepare_s()
        for i in (4, 5):
            widen_x(i)
            turn_x(i)
        permute_w_codes(1)
        permute_w_scales(1)
        embed(0, 0)
        for i in (4, 5):
            scale_x(i)
        for i in (6, 7):
            widen_x(i)
        embed(0, 1)
        prepare_psi()
        for i in (6, 7):
            turn_x(i)
        gain_z(0, 0)
        for i in (6, 7):
            scale_x(i)
        quantise_x(1)
        embed(1, 0)
        gain_z(0, 1)
        finish_psi()
        quantise_z(0, 0)
        embed(1, 1)
        quantise_z(0, 1)
        for j in range(EARLY):
            multiply_a(j, 0)
        gain_z(1, 0)
        for j in range(EARLY):
            count_turns(j, 0)
        for j in range(EARLY):
            take_turns(j, 0)
            find_sizes(j, 0, HALF)
            find_sines(j, 0, HALF)
            find_cosines(j, 0, HALF)
        gain_z(1, 1)
        quantise_z(1, 0)
        quantise_z(1, 1)

        def halves_left(j):
            return [1] if j < EARLY else [0, 1]

        coming = [(j, h) for j in range(SLICE_TILES) for h in halves_left(j)]
        for n in range(2):
            multiply_a(*coming.pop(0))
        for j in range(SLICE_TILES):
            last = j == SLICE_TILES - 1
            for h in halves_left(j):
                count_turns(j, h)
            for h in halves_left(j):
                take_turns(j, h)
            lo = HALF if j < EARLY else 0
            find_sizes(j, lo, ROWS)
            find_sines(j, lo, ROWS)
            if last:
                find_cosine_factor(j)
                for h in range(HALVES):
                    find_cosines(j, HALF * h, HALF * (h + 1))
            else:
                find_cosines(j, lo, ROWS)
                find_cosine_factor(j)
            find_sine_factor(j)
            if j < SLICE_TILES - VECTOR_TILES:
                weigh(nc.gpsimd, j, 0, ROWS)
            for h in range(HALVES):
                if j >= LEAVE_LAG:
                    leave(nc.vector.tensor_copy, j - LEAVE_LAG, h)
            for h in range(HALVES):
                if coming:
                    multiply_a(*coming.pop(0))
                if j >= TURN_LAG:
                    turn_out(j - TURN_LAG, h)

        before, last = SLICE_TILES - 2, SLICE_TILES - 1
        for j in range(SLICE_TILES - TURN_LAG, before):
            for h in range(HALVES):
                turn_out(j, h)
        weigh(nc.vector, before, 0, ROWS)
        for h in range(HALVES):
            turn_out(before, h)
        for j in range(SLICE_TILES - LEAVE_LAG, before):
            for h in range(HALVES):
                leave(nc.vector.tensor_copy, j, h)
        leave(nc.vector.tensor_copy, before, 0)
        for h in range(HALVES):
            weigh(nc.vector, last, HALF * h, HALF * (h + 1))
            turn_out(last, h)
        leave(nc.scalar.copy, before, 1)
        leave(nc.scalar.copy, last, 0)
        leave(nc.vector.tensor_copy, last, 1)
